import numpy as np, ml_dtypes
CORES = [40,64,80,88,96,104,120,144]
N = 8
import mx_ref
BF = ml_dtypes.bfloat16
def gentries(a):
    return np.ascontiguousarray(a.reshape(8, 16, -1).transpose(0, 2, 1)).reshape(8, -1)
def gtable(e):
    e = np.asarray(e); return np.ascontiguousarray(e.reshape(8, -1, 16).transpose(0, 2, 1)).reshape(128, -1).astype(np.int32)
def gcols(t, e):
    v = np.concatenate([t.reshape(8, 16, -1, 4), np.zeros((8, 16, 1, 4), BF)], axis=2)
    return np.ascontiguousarray(np.stack([v[g][:, e[g]] for g in range(8)])).reshape(128, -1)
def tile(rs):
    return np.stack(rs, axis=2).reshape(128, -1).astype(BF)
def pick(q, e):
    c = np.concatenate([q[0].reshape(128, -1, 4), np.zeros((128, 1, 4), np.uint8)], axis=1); s = np.concatenate([q[1], np.ones((16, 1), np.uint8)], axis=1)
    return (np.ascontiguousarray(c[:, e].reshape(128, -1)), np.ascontiguousarray(s[:, e]))
def join(*qs):
    return (np.concatenate([q[0] for q in qs], axis=1), np.concatenate([q[1] for q in qs], axis=1))
def put(q, e, v):
    c, s = q[0].reshape(128, -1, 4).copy(), q[1].copy(); c[:, e] = v[0].reshape(128, -1, 4); s[:, e] = v[1]
    return (c.reshape(128, -1), s)
def pk(c, s):
    return (np.ascontiguousarray(c), mx_ref.live(s))
def emit(q):
    return q[0], q[1]
def packed(v, rng):
    q = [mx_ref.quantize(np.ascontiguousarray(v[r])) for r in range(N)]
    return np.stack([a for a, b in q]), np.stack([mx_ref.plane(b, rng) for a, b in q])
def values_of_codes():
    e, c = np.zeros((128, 128, 4), np.float32), np.zeros((128, 2, 4), np.uint8)
    e[np.arange(128), np.arange(128), 0] = 1
    c[:127, :, 0] = np.arange(256).reshape(2, 128).T[:127]
    return mx_ref.matmul(mx_ref.quantize(e.reshape(128, 512).astype(BF)), (c.reshape(128, 8), np.full((16, 2), 127, np.uint8))).T.reshape(-1).astype(np.float64)
CODE_VALUE, SCALE_VALUE = values_of_codes(), 2.0 ** (np.arange(256) - 127.0)
def decode(q):
    return (CODE_VALUE[q[0]].reshape(16, 8, -1, 4) * SCALE_VALUE[q[1]][:, None, :, None] + 0.0).reshape(128, -1).astype(np.float32)
def f(rng, *shape):
    return mx_ref.flush((rng.standard_normal(shape, dtype=np.float32) * np.exp2(rng.integers(-2, 3, shape[:-1] + (1,)))).astype(BF))
def wide(rng, *shape, cols=0):
    v = rng.standard_normal(shape, dtype=np.float32) * np.exp2(rng.integers(-12, 13, shape)).astype(np.float32)
    if cols: v *= np.repeat(np.exp2(rng.integers(-cols, cols + 1, shape[:-2] + (1, shape[-1] // 4))) * (rng.random(shape[:-2] + (1, shape[-1] // 4)) > 0.0625), 4, axis=-1).astype(np.float32)
    return mx_ref.flush(v.astype(BF))
C, HALF = 352, 176
STEP = [1, 2, 4]
def numbers_of(rng):
    return {"x": np.array(f(rng, N, 128, 4 * C)), "lv": np.array(f(rng, N, 128, 4 * C)), "u": np.array(f(rng, N, 128, 512)), "v": np.array(f(rng, N, 128, 512))}
def names(rng):
    return rng.permuted(np.tile(np.arange(2 * C), (N, 8, 1)), axis=2)
def paired(rng, roots):
    p, n = np.flatnonzero(roots), np.flatnonzero(~roots)
    k = np.zeros(2 * C, np.int64)
    k[p] = rng.permutation(n)
    k[np.concatenate([n, np.arange(C, 2 * C)])] = rng.permutation(np.concatenate([p, np.arange(C, 2 * C)]))
    return k
def stored(k):
    return {"lt": np.stack([gtable(k[r][:, :C]) for r in range(N)]), "rt": np.stack([gtable(k[r][:, C:]) for r in range(N)])}
def layers(rng):
    return np.array(f(rng, N, 128, 2048)).reshape(N, 8, 16, 4, 8, 16, 4)
def weights(rng, w):
    c, p = packed(np.ascontiguousarray(w).reshape(N, 128, 2048), rng)
    return {"wc": c, "ws": p}
def setup_inputs(rng):
    return {**numbers_of(rng), **stored(names(rng)), **weights(rng, layers(rng))}
def setup_inputs_ties(rng):
    d = numbers_of(rng)
    o = rng.permutation(N)
    k = rng.integers(-1, 2, (N, 8, 4, C)).astype(np.float32)
    k[o[1]] = 1
    e = names(rng)
    for g in range(8):
        p = rng.permutation(C) < HALF
        k[o[3], g, 0] = np.where(p, 1.0, -1.0)
        if g % 2:
            k[o[3], g, 1] = np.minimum(k[o[3], g, 1], 0)
            k[o[3], g, 2] = k[o[3], g, 0]
        e[o[3], g] = paired(rng, p)
    x = d["x"].reshape(N, 8, 16, C, 4)
    x[:, :, :8] = 0
    x[:, :, :4, :, 0] = k.astype(BF)
    c = np.ones(N, np.float32)
    c[o[0]] = 0
    c[o[2]] = -1
    u = d["u"].reshape(N, 128, 128, 4)
    for g in range(8):
        for h in range(16 * g, 16 * g + 4):
            u[:, :, h] = 0
            u[:, h, h, 0] = c.astype(BF)
    w = layers(rng)
    w[:, :, :, :, :, :8] = 0
    return {"x": x.reshape(N, 128, 4 * C), "lv": d["lv"], "u": u.reshape(N, 128, 512), "v": d["v"], **stored(e), **weights(rng, w)}
def setup_inputs_near(rng):
    d = numbers_of(rng)
    o = rng.permutation(N)
    t = int(np.flatnonzero(o == 0)[0])
    k = np.where(o % 2 == 0, 2.0 ** -30, 1.0).astype(np.float32)
    x = d["x"].astype(np.float32).reshape(N, 8, 16, C, 4)
    lv = d["lv"].astype(np.float32).reshape(N, 8, 16, C, 4)
    s = rng.integers(-1, 2, (N, 8, 4, C)) * np.where(o % 2 == 0, 2.0 ** -28, 1.0)[:, None, None, None]
    x[:, :, :8] = 0
    x[:, :, :4, :, 0] = 1.125 * s
    x[:, :, 4:8, :, 0] = -1.25 * s
    for r in range(N):
        at = [0, C - 1, int(rng.integers(C)), int(rng.integers(C))]
        for g, j in zip(rng.permutation(8)[:4], at): x[r, g, rng.integers(4), j, 0] = 2.0 ** 30 * rng.choice([-1.0, 1.0])
    x[t] = 0
    x[t, :, 7, :, 3] = 2.0 ** -29
    for z in (x, lv):
        z[:, :, 15, :, 3] = 4.0
        z[t, :, 8:] = rng.choice([-1.0, 1.0], (8, 8, C, 4)) * 2.0 ** -26
        z[t, :, 8:12, :, 0] *= np.float32(2.0 ** -4)
        z[t, ::2, 9:12:2, :, 0] = 2.0 ** -30
        z[t, :, 15, :, 3] = 2.0 ** -28
    u = d["u"].reshape(N, 128, 128, 4)
    w = layers(rng)
    w[:, :, :8] = 0
    w[:, :, :, :, :, :8] = 0
    w[:, :, :, 3, :, 15] = 0
    w[:, :, 15, 3, :, 15, 3] = 4.0
    w[t, :, 15, 3, :, 7, 3] = 4.0
    for g in range(8):
        for i in range(4):
            h = 16 * g + i
            u[:, :, h] = 0
            u[:, h, h, 0] = (1.125 * k).astype(BF)
            u[:, h + 4, h, 0] = k.astype(BF)
            u[t, :, h] = 0
            u[t, h, h, 1] = 1.125 * 2.0 ** -30
            u[t, h + 4, h, 1] = 2.0 ** -30
            w[t, g, 8 + i, 1, g, i, 0] = 1.125 * 2.0 ** -5
            w[t, g, 8 + i, 1, g, i + 4, 0] = -1.25 * 2.0 ** -5
    return {"x": x.reshape(N, 128, 4 * C).astype(BF), "lv": lv.reshape(N, 128, 4 * C).astype(BF), "u": u.reshape(N, 128, 512), "v": d["v"], **stored(names(rng)), **weights(rng, w)}
def setup_inputs_odd(rng):
    d = numbers_of(rng)
    x = np.zeros((N, 8, 16, C, 4), np.float32)
    lv = np.zeros((N, 8, 16, C, 4), np.float32)
    a = np.exp2(rng.integers(5, 9, (8, 1)).astype(np.float32))
    b = rng.integers(0, 2, (N, 8, 4, C))
    x[:, :, 0, :, 3] = 1.96875 * 2.0 ** 8
    x[:, :, 0:8:2, :, 0] = (8 + b) * 2.0 ** -8
    x[:, :, 1:8:2, :, 0] = (9 - b) * 2.0 ** -8
    for t in (x, lv):
        t[:, :, 7, :, 1] = 1.125 * a
        t[:, :, 7, :, 2] = 0.0703125 * a
    x[:, :, 9, :, 0] = -a
    u = d["u"].reshape(N, 128, 128, 4)
    w = np.zeros((N, 8, 16, 4, 8, 16, 4), np.float32)
    for g in range(8):
        w[:, g, 7, 0, g, 9, 1] = 28.0
        for i in range(4):
            u[:, :, 16 * g + i] = 0
            u[:, 16 * g + 2 * i, 16 * g + i, 0] = 1.0
            u[:, 16 * g + 2 * i + 1, 16 * g + i, 0] = -1.0
            w[:, g, 7, i, g, 10, 2] = [1.0, 1.25, 0.75, 0.5625][i] * 2.0 ** -5
    return {"x": x.reshape(N, 128, 4 * C).astype(BF), "lv": lv.reshape(N, 128, 4 * C).astype(BF), "u": u.reshape(N, 128, 512), "v": d["v"], **stored(names(rng)), **weights(rng, w.astype(BF))}
def setup_inputs_ends(rng):
    d = numbers_of(rng)
    n = np.arange(N)
    o = np.array([1, 0, 2, 3])[(n & 3) ^ rng.integers(0, 4, 2)[n >> 2]]
    x = np.zeros((N, 8, 16, C, 4), np.float32)
    lv = np.zeros((N, 8, 16, C, 4), np.float32)
    a = np.zeros((N, 8, 4))
    k = names(rng)
    w = np.zeros((N, 128, 4, 128, 4), np.float32)
    i, c = np.arange(128), np.arange(C)
    for r in range(N):
        a[r] = rng.choice([-1.0, 1.0], (8, 4)) * (rng.permutation(8) > 1)[:, None]
        roots = rng.permutation(C) < HALF
        s = rng.choice([-1.0, 1.0], (2, 8, 16, C, 4))
        size = (0.6 + 0.05 * rng.random((2, 8, 16, C, 4))) * 2.0 ** 30
        if o[r] == 0:
            s[:] = -1.0
            k[r] = np.concatenate([2 * C - 1 - c, C - 1 - c])
        if o[r] == 1:
            s[0] = np.where(roots, 1.0, -1.0)[None, None, :, None]
            for g in range(8): k[r, g] = paired(rng, ~roots if a[r, g, 0] < 0 else roots)
        if o[r] == 2: k[r] = np.concatenate([(c + 1) % C, 2 * C - 1 - c])
        if o[r] == 3:
            s[0] = s[0][:, :1, :, :1]
            size[:] = 2.0 ** -28
            for j, g in enumerate(rng.permutation(8)):
                k[r, g] = np.concatenate([rng.permutation(C) + C * (j % 2), rng.permutation(C) + C * (1 - j % 2)])
        x[r], lv[r] = s * size
        if o[r] == 2: w[r] = rng.choice([-1.0, 1.0], (128, 4, 128, 4)) * 2.0 ** -6
        else:
            for b in range(4): w[r, i, b, i, b] = -1.0 if o[r] < 2 else 64.0
    size = np.where(o == 3, 2.0 ** -30, 2.0 ** 30)
    u = d["u"].reshape(N, 128, 128, 4)
    for j in range(4): u[:, :, j::16] = (a[:, :, j] * size[:, None] + 0.0).astype(np.float32).astype(BF)[:, None, :, None]
    v = rng.choice([-1.0, 1.0], (N, 128, 512)) * size[:, None, None]
    return {"x": x.reshape(N, 128, 4 * C).astype(BF), "lv": lv.reshape(N, 128, 4 * C).astype(BF), "u": u.reshape(N, 128, 512), "v": v.astype(np.float32).astype(BF), **stored(k), **weights(rng, w.astype(BF))}
def setup_inputs_spread(rng):
    d = setup_inputs(rng)
    d["x"] = wide(rng, N, 128, 4 * C, cols=6)
    d["lv"] = wide(rng, N, 128, 4 * C, cols=6)
    return d
def check_inputs(d):
    b = []
    for k in ("x", "lv", "u", "v"):
        a = np.abs(d[k].astype(np.float32))
        if not (np.isfinite(a).all() and ((a == 0) | (a >= 2.0 ** -30) & (a <= 2.0 ** 30)).all()): b.append("a value of " + k)
    none, least, most = [emit(mx_ref.quantize(np.full((128, 16), k, np.float32).astype(BF)))[1][0, 0] for k in (0.0, 2.0 ** -6, 2.0 ** 6)]
    for r in range(N):
        if (np.sort(np.concatenate([gentries(d["lt"][r]), gentries(d["rt"][r])], axis=1), axis=1) != np.arange(2 * C)).any(): b.append("lt and rt: not every name once in a group")
        if ((d["wc"][r] == 0x7F) | (d["wc"][r] == 0xFF)).any(): b.append("wc: a code that is no number")
        s = mx_ref.live(d["ws"][r])
        if ((s != none) & ((s < least) | (s > most))).any(): b.append("ws: a scale out of range")
        if (((d["wc"][r].reshape(16, 8, 512, 4) & 0x7F) != 0) & (s == none)[:, None, :, None]).any(): b.append("wc: a code other than zero under the scale of zeros")
    return b
def rewrite(left, right, act, turn):
    g, c = np.nonzero((left < C) & (act > 0) & (np.take_along_axis(act, left % C, 1) < 0))
    s = left[g, c]
    a, b, z = left[g, s], right[g, s], right[g, c]
    t = turn[g, a % C] > 0
    left, right = left.copy(), right.copy()
    left[g, c], right[g, c] = np.where(t, a, s), np.where(t, s, b)
    left[g, s], right[g, s] = np.where(t, b, a), z
    return left, right
def reference(x, lv, u, v, lt, rt, wc, ws):
    qu = [mx_ref.quantize(u[r]) for r in range(N)]
    lay = [pk(wc[r], ws[r]) for r in range(N)]
    left, right = [gentries(lt[r]) for r in range(N)], [gentries(rt[r]) for r in range(N)]
    now, leaf = [x[r] for r in range(N)], [lv[r] for r in range(N)]
    for step in STEP:
        made = []
        for r in range(N):
            s = mx_ref.matmul(qu[r], mx_ref.quantize(now[r])).reshape(8, 16, C)
            for j in range(2): left[r], right[r] = rewrite(left[r], right[r], s[:, 2 * j], s[:, 2 * j + 1])
            win = np.concatenate([now[r], leaf[r]], axis=1)
            z = mx_ref.quantize(((gcols(win, left[r]).astype(np.float32) + gcols(win, right[r]).astype(np.float32)) * np.float32(0.5)).astype(BF))
            made.append(tile([mx_ref.matmul(pick(lay[r], np.arange(128 * b, 128 * b + 128)), z) * np.float32(0.03125) for b in range(4)]))
        for r in range(N):
            p = r ^ step
            m = np.take_along_axis(left[p], right[r] % C, 1) % C
            far = gcols(decode(mx_ref.quantize(made[p])).astype(BF), m[:, :HALF])
            leaf[r] = np.concatenate([far, gcols(made[r], m[:, HALF:])], axis=1)
            now[r] = (now[r].astype(np.float32) + leaf[r].astype(np.float32)).astype(BF)
    y, gr = np.zeros((N, 128, C), np.float32), np.zeros((N, 8, 2 * C), np.float32)
    oc, osc = np.zeros((N, 128, 4 * C), np.uint8), np.zeros((N, 16, C), np.uint8)
    for r in range(N):
        q = mx_ref.quantize(now[r])
        y[r] = mx_ref.matmul(mx_ref.quantize(v[r]), q)
        gr[r] = np.concatenate([left[r], right[r]], axis=1)
        oc[r], osc[r] = emit(q)
    return {"y": y, "gr": gr, "oc": oc, "osc": osc}

@@ -1,0 +1,520 @@
+from concourse.bass import DstId, RemoteDMATransfer
+from concourse.mybir import dt, AluOpType, ActivationFunctionType
+
+Op, Act = AluOpType, ActivationFunctionType
+C, HALF, K = 352, 176, 22
+STEP = [1, 2, 4]
+F21, F10 = 2.0 ** -21, 2.0 ** 10
+CHUNKS = [(0, 192), (192, 352)]
+WIDE = [("LR0", 44), ("LR1", 44), ("CB", 44), ("F", 66), ("LH", 44), ("D", 44), ("E", 44), ("Q", 44), ("SS", 44), ("M1", 44), ("M2", 44), ("M3", 44),
+        ("N1", 44), ("N2", 44), ("N3", 44), ("N4", 44), ("t1", 44), ("t2", 44), ("par", 22), ("x", 22), ("i32", 22), ("A", 22), ("dlp", 22), ("aM", 22),
+        ("o", 22), ("I", 22), ("vA", 22), ("vN", 22), ("mi", 22), ("mt", 22), ("mm", 22)]
+U16S = [("OL0", 44), ("OL1", 22), ("OLC0", 22), ("OLC1", 22), ("O", 22), ("SL0", 44), ("SL1", 44), ("LX", 22), ("MO", 22)]
+FTHS = [("tA", 22), ("tP", 22), ("tN", 22), ("tQ", 22), ("pk", 22), ("px", 8)]
+
+
+def places(blocks):
+    at, d = 0, {}
+    for n, w in blocks:
+        d[n] = at
+        at += (w + 7) // 8 * 8
+    return d, at
+
+
+WI, WIN_ = places(WIDE)
+WU, WUN = places(U16S)
+WF, WFN = places(FTHS)
+
+
+def codes_of(name, n):
+    return {"q" + name: ("sbuf", [128, n], "float8_e4m3fn_x4"), "s" + name: ("sbuf", [128, n], "uint8")}
+
+
+def tiles(kind, **widths):
+    return {k: ("sbuf", [128, w], kind) for k, w in widths.items()}
+
+
+SCRATCH = {
+    **tiles("bfloat16", xt=4 * C, lvt=4 * C, ut=512, vt=512, win=8 * C, gl=4 * C, zt=4 * C, hp=4 * C, gt=4 * HALF, et=2048, one=512),
+    **codes_of("x", C), **codes_of("u", 128), **codes_of("ur", 512), **codes_of("v", 128), **codes_of("w", 512), **codes_of("e", 512), **codes_of("z", C),
+    **tiles("int32", lw=K, rw=K, wi=WIN_, ui=32, ri=C),
+    **tiles("uint16", wu=WUN, ux=32),
+    **tiles("float32", wf=WFN, ones=32, ex=704, tr=704, kr=C, dm=C, km=C, rc=C, none=C, wa=4 * C, wb=2 * C, lrf=C, lrs=C, a1=C, tw0=2 * C, tw1=2 * C,
+            pw0=2 * C, pw1=2 * C, sg0=C, sg1=C, sgt=C, pf0=C, pf1=C, e1=C, e2=C, gg=C, e3=C, gro=2 * C, yo=C),
+}
+for _b in range(8):
+    SCRATCH["ps%d" % _b] = ("psum", [128, 512], "float32")
+for _r in range(3):
+    for _n in ("so", "ro", "la"):
+        SCRATCH["%sR%d" % (_n, _r)] = ("sbuf", [128, 2 * K if _n == "so" else K], "uint16")
+        SCRATCH["%sM%d" % (_n, _r)] = ("sbuf", [128, 11], "uint16")
+        SCRATCH["%sQ%d" % (_n, _r)] = ("sbuf", [128, HALF], "float8_e4m3fn_x4")
+        SCRATCH["%sS%d" % (_n, _r)] = ("sbuf", [128, HALF], "uint8")
+LOADS = ["lt", "rt", "x", "u", "lv", "wc", "ws", "v"]
+SEMAPHORES = (["cv", "cs", "ct", "cp", "ls", "outs"] + ["ld_" + n for n in LOADS]
+              + ["a%s%d" % (n, r) for n in "RMCS" for r in range(3)])
+
+
+def route(topo, core, partner):
+    ok = [c for c in topo.cores_of(core) if c != core and topo.may_write(c, partner)]
+    near = [c for c in ok if topo.die(c) == topo.die(core)]
+    far = [c for c in ok if topo.die(c) != topo.die(core)]
+    return near[0], far[0], near[1]
+
+
+def bits(engines):
+    return sum(1 << e for e in engines)
+
+
+def relay_program(g, core, T, topo, rank):
+    src, sent = T.cores[rank], 0
+    for rd, s in enumerate(STEP):
+        dst = T.cores[rank ^ s]
+        a, b, c = route(topo, src, dst)
+        if core not in (a, b, c):
+            continue
+        rid, pid = topo.addr(dst, core)
+        eng = topo.engines(core, dst)[:8]
+        jobs = {a: [("R", "R", 0, K), ("C", "Q", 0, 88)], b: [("C", "Q", 88, HALF)], c: [("M", "M", 0, 11), ("S", "S", 0, HALF)]}[core]
+        for sem, buf, lo, hi in jobs:
+            g.wait_ge(T.sem["a%s%d" % (sem, rd)], 8)
+            o, i = T["la%s%d" % (buf, rd)][:, lo:hi], T["ro%s%d" % (buf, rd)][:, lo:hi]
+            if buf == "Q":
+                o, i = o.bitcast(dt.uint8), i.bitcast(dt.uint8)
+            g.remote_dma(o, i, T.sem["a%s%d" % (sem, rd)], T.sem["ls"], pid, rid, bits(eng))
+            sent += len(eng)
+    if sent:
+        g.wait_ge(T.sem["ls"], sent)
+
+
+def rank_program(g, core, T, topo):
+    rank = T.rank_of(core)
+    if rank is None:
+        for c in topo.cores_of(core):
+            if T.rank_of(c) is not None:
+                relay_program(g, core, T, topo, T.rank_of(c))
+        return
+
+    eng = {"v": g.vector, "s": g.scalar, "t": g.tensor, "p": g, "y": g.sync}
+    done = {"v": "cv", "s": "cs", "t": "ct", "p": "cp"}
+    count = {"cv": 0, "cs": 0, "ct": 0, "cp": 0, "outs": 0, "ls": 0}
+    known = {q: {} for q in eng}
+    uses = {}
+    clocks = {}
+
+    def meet(a, b):
+        if a[1] >= b[2] or b[1] >= a[2]:
+            return False
+        return not (a[3] == b[3] and a[3] > 1 and (a[1] - b[1]) % a[3])
+
+    def before(q, reads, writes):
+        need = {}
+        for w, regs in ((False, reads), (True, writes)):
+            for r in regs:
+                ps = r[0][:2] == "ps"
+                for (o, ow, oq, tok) in uses.get(r[0], []):
+                    if (w or ow or (ps and oq != q)) and meet(r, o):
+                        need[tok[0]] = max(need.get(tok[0], 0), tok[1])
+        k = known[q]
+        for s in sorted(need, key=lambda s: s in ("cv", "cs", "ct", "cp")):
+            if k.get(s, 0) < need[s]:
+                eng[q].wait_ge(T.sem[s], need[s])
+                k[s] = need[s]
+                for a, b in clocks.get((s, need[s]), {}).items():
+                    k[a] = max(k.get(a, 0), b)
+
+    def note(q, tok, reads, writes):
+        clocks[tok] = dict(known[q])
+        for r in writes:
+            uses[r[0]] = [u for u in uses.get(r[0], []) if not (r[3] in (1, u[0][3]) and r[1] <= u[0][1] and u[0][2] <= r[2] and (u[0][1] - r[1]) % r[3] == 0)]
+        for w, regs in ((False, reads), (True, writes)):
+            for r in regs:
+                uses.setdefault(r[0], []).append((r, w, q, tok))
+
+    def run(q, fn, reads, writes):
+        before(q, reads, writes)
+        s = done[q]
+        count[s] += 1
+        fn().then_inc(T.sem[s], 1)
+        note(q, (s, count[s]), reads, writes)
+
+    def load(q, sem, out, in_, reg):
+        before(q, [], [reg])
+        eng[q].dma_start(out, in_).then_inc(T.sem[sem], 16)
+        note(q, (sem, 16), [], [reg])
+
+    def store(q, out, in_, reg):
+        before(q, [reg], [])
+        eng[q].dma_start(out, in_).then_inc(T.sem["outs"], 16)
+        count["outs"] += 16
+
+    def R(name, lo=0, hi=None, step=1):
+        return (name, lo, SCRATCH[name][1][1] if hi is None else hi, step)
+
+    def W(name, lo=0, hi=K):
+        return ("wi", WI[name] + lo, WI[name] + hi, 1)
+
+    def U(name, lo=0, hi=K):
+        return ("wu", WU[name] + lo, WU[name] + hi, 1)
+
+    def Fl(name, lo=0, hi=K):
+        return ("wf", WF[name] + lo, WF[name] + hi, 1)
+
+    def ap(r):
+        return T[r[0]][:, r[1]:r[2]] if r[3] == 1 else T[r[0]][:, r[1]:r[2]:r[3]]
+
+    def src(r, ind):
+        return ap(r) if ind is None else ap(r).indirect(ap(ind))
+
+    def given(*rs):
+        return [r for r in rs if r is not None]
+
+    def tt(out, in0, in1, op, ind=None):
+        run("v", lambda: g.vector.tensor_tensor(ap(out), src(in0, ind), ap(in1), op), given(in0, in1, ind), [out])
+
+    def ts(out, in0, s1, op0, s2=None, op1=None):
+        if op1 is None:
+            run("v", lambda: g.vector.tensor_scalar(ap(out), ap(in0), s1, None, op0), [in0], [out])
+        else:
+            run("v", lambda: g.vector.tensor_scalar(ap(out), ap(in0), s1, s2, op0, op1), [in0], [out])
+
+    def cp(out, in_, ind=None):
+        run("v", lambda: g.vector.tensor_copy(ap(out), src(in_, ind)), given(in_, ind), [out])
+
+    def put(out, ind, in_):
+        run("v", lambda: g.vector.tensor_copy(ap(out).indirect(ap(ind)), ap(in_)), [in_, ind], [out])
+
+    def fill(out, c):
+        run("v", lambda: g.vector.memset(ap(out), c), [], [out])
+
+    def act(out, in_, ind=None, func=Act.Copy, scale=1.0):
+        if scale == 1.0:
+            run("s", lambda: g.scalar.activation(ap(out), src(in_, ind), func), given(in_, ind), [out])
+        else:
+            run("s", lambda: g.scalar.activation(ap(out), src(in_, ind), func, scale=scale), given(in_, ind), [out])
+
+    def scan(out, d0, d1, op0, op1):
+        run("v", lambda: g.vector.tensor_tensor_scan(ap(out), ap(d0), ap(d1), 0.0, op0, op1), [d0, d1], [out])
+
+    def quant(name, tile, lo, hi, q=None, s=None):
+        q, s = q or "q" + name, s or "s" + name
+        t = R(tile, 4 * lo, 4 * hi)
+        run("v", lambda: g.vector.quantize_mx(T[q][:, lo:hi], T[s][:, lo:hi], ap(t)), [t], [R(q, lo, hi), R(s, lo, hi)])
+
+    def mm(bank, w, wlo, q, s, lo, hi):
+        p, wq, wsc = "ps%d" % bank, "q" + w, "s" + w
+        run("t", lambda: g.tensor.matmul_mx(T[p][:, 0:hi - lo], T[wq][:, wlo:wlo + 128], T[wsc][:, wlo:wlo + 128], T[q][:, lo:hi], T[s][:, lo:hi], True, True),
+            [R(wq, wlo, wlo + 128), R(wsc, wlo, wlo + 128), R(q, lo, hi), R(s, lo, hi)], [R(p)])
+
+    def arrive(name, sem, n):
+        note("p", (sem, n), [], [R(name)])
+        clocks[(sem, n)] = {}
+
+    def send(rds, fn, n):
+        before("p", rds, [])
+        fn()
+        count["ls"] += n
+
+    def masked(out, row):
+        scan(out, row, R("dm"), Op.add, Op.mult)
+
+    def pick(out, row):
+        scan(out, R("km"), row, Op.mult, Op.add)
+
+    def ends(name):
+        return (name, 15, C, 16)
+
+    def col16(out, x):
+        w = x[2] - x[1]
+        ts(W("t1", 0, w), x, float(C), Op.is_ge, -float(C), Op.mult)
+        tt(W("t2", 0, w), x, W("t1", 0, w), Op.add)
+        cp(out, W("t2", 0, w))
+
+    def iota(out, pattern, base, cm):
+        if out[0] in ("kr", "rc"):
+            run("p", lambda: g.iota(ap(out), pattern, base, cm, allow_small_or_imprecise_dtypes=True), [], [out])
+        else:
+            run("p", lambda: g.iota(ap(out), pattern, base, cm), [], [out])
+
+    load("y", "ld_lt", T["lw"][:], T["lt"][:], R("lw"))
+    load("s", "ld_rt", T["rw"][:], T["rt"][:], R("rw"))
+    load("y", "ld_u", T["ut"][:], T["u"][:], R("ut"))
+    load("s", "ld_x", T["xt"][:], T["x"][:], R("xt"))
+    load("y", "ld_lv", T["lvt"][:], T["lv"][:], R("lvt"))
+    load("y", "ld_wc", T["qw"][:, 0:512].bitcast(dt.uint8), T["wc"][:, 0:2048], R("qw"))
+    load("y", "ld_ws", T["sw"][:, 0:512], T["ws"][:, 0:512], R("sw"))
+    load("y", "ld_v", T["vt"][:], T["v"][:], R("vt"))
+
+    iota(W("x"), [[0, K]], 0, 1)
+    iota(R("kr"), [[0, K], [1, 16]], 0, 0)
+    iota(W("i32"), [[32, K]], 0, 0)
+    iota(W("mm"), [[16, K]], 0, 0)
+    iota(R("ui"), [[1, 4], [16, 8]], 0, 0)
+    iota(R("rc"), [[1, C]], 0, 0)
+    fill(R("none"), float(C))
+    fill(R("ones"), 1.0)
+    fill(R("km"), 1.0)
+    fill(W("SS"), C)
+    act(R("pw0", 0, C), R("none"))
+    ts(W("t1"), W("x"), 31, Op.bitwise_and)
+    ts(W("t2"), W("x"), 15, Op.bitwise_and)
+    fill(R("km", 0, C, 16), 0.0)
+    cp(Fl("px", 0, 8), W("t2", 0, 8))
+    tt(W("mt"), W("t1"), W("i32"), Op.add)
+    px = Fl("px", 0, 1)
+    run("v", lambda: g.vector.tensor_scalar(T["dm"][:], T["kr"][:], ap(px), None, Op.is_equal), [R("kr"), px], [R("dm")])
+    cp(U("LX"), W("mt"))
+    tt(W("CB"), W("t2"), W("mm"), Op.add)
+    cp(R("ux"), R("ui"))
+    ts(W("CB", K, 2 * K), W("CB"), float(C), Op.add)
+
+    ts(W("mi"), R("rw"), 1024.0, Op.mult)
+    cp(U("OL0"), R("lw"))
+    tt(Fl("pk"), W("mi"), R("lw"), Op.add)
+    for q in range(K):
+        o, i = R("ex", 32 * q, 32 * q + 32), Fl("pk", q, q + 1)
+        run("s", lambda: g.scalar.activation(ap(o), T["ones"][:], Act.Copy, scale=ap(i)), [R("ones"), i], [o])
+    fill(R("tw0", C, 2 * C), 0.0)
+    quant("u", "ut", 0, 128)
+
+    def replicas(k):
+        a, e = 128 * k, 8 * k
+        run("v", lambda: g.vector.tensor_copy(T["qur"][:, a:a + 256].bitcast(dt.uint32), T["qu"][:, 0:128].bitcast(dt.uint32).indirect(T["ux"][:, e:e + 16])),
+            [R("qu"), R("ux")], [R("qur", a, a + 256)])
+        run("s", lambda: g.scalar.activation(T["sur"][:, a:a + 256], T["su"][:, 0:128].indirect(T["ux"][:, e:e + 16]), Act.Copy),
+            [R("su"), R("ux")], [R("sur", a, a + 256)])
+
+    def parents(pw, ol):
+        put(R(pw), ol, R("rc"))
+        masked(R("e1"), R(pw, 0, C))
+        pick(R("e2"), R("e1"))
+        cp(W("par"), ends("e2"))
+
+    replicas(0)
+    run("v", lambda: g.vector.transpose(T["tr"][:], T["ex"][:]), [R("ex")], [R("tr")])
+    act(R("lrf"), R("tr"), U("LX"), scale=F21)
+    fill(R("one"), 1.0)
+    cp(W("LR0"), R("lw"))
+    cp(W("LR0", K, 2 * K), R("rw"))
+    col16(U("OLC0"), W("LR0"))
+    quant("x", "xt", 0, C)
+    parents("pw0", U("OL0"))
+    fill(R("tw1", C, 2 * C), 0.0)
+    for b in range(4):
+        run("p", lambda: g.affine_select(T["et"][:, 512 * b:512 * b + 512], T["one"][:], [[-1, 512]], Op.is_equal, 0.0, b, 4),
+            [R("one")], [R("et", 512 * b, 512 * b + 512)])
+
+    def windows():
+        for t in range(4):
+            act(R("win", 704 * t, 704 * t + C), R("xt", t, 4 * C, 4), scale=0.5)
+
+    def signs(lo, hi, bank):
+        for k in range(2):
+            mm(bank + k, "ur", 128 * k, "qx", "sx", lo, hi)
+        act(R("sg0", lo, hi), R("ps%d" % bank, 0, hi - lo), func=Act.Sign, scale=-1.0)
+        ts(R("pf0", lo, hi), R("ps%d" % (bank + 1), 0, hi - lo), 0.0, Op.is_gt, 0.5, Op.mult)
+        tt(R("lrs", lo, hi), R("lrf", lo, hi), R("sg0", lo, hi), Op.add)
+
+    def step(rd, j, more=None):
+        lr, ln = W("LR%d" % j, 0, 44), W("LR%d" % (1 - j), 0, 44)
+        l, r = W("LR%d" % j), W("LR%d" % j, K, 2 * K)
+        olc, tw, pf = U("OLC%d" % j), "tw%d" % j, R("pf%d" % j)
+        sl, sr = U("SL0", 0, K), U("SL0", K, 2 * K)
+        if j == 0:
+            tt(R(tw, 0, C), pf, R("lrs"), Op.add, olc)
+            more()
+        else:
+            tt(R(tw, 0, C), pf, R("lrs"), Op.add, olc)
+            act(R("wb", 0, C), R("wa", 0, 2 * C), sl)
+            act(R("wb", C, 2 * C), R("wa", 0, 2 * C), sr)
+            parents("pw1", U("OL1"))
+        masked(R("e1"), R(tw, 0, C))
+        tt(W("dlp"), l, W("par"), Op.subtract)
+        tt(W("E"), r, l, Op.subtract)
+        tt(W("Q"), l, W("CB"), Op.subtract)
+        pick(R("e2"), R("e1"))
+        own = ends("e2")
+        ts(W("A"), own, 0.0, Op.is_lt)
+        tt(W("aM"), W("A"), W("dlp"), Op.mult)
+        tt(W("o"), W("aM"), W("par"), Op.add)
+        cp(U("O"), W("o"))
+        tt(R("gg"), R(tw), R("dm"), Op.mult, U("O"))
+        ts(Fl("tP"), own, 0.0, Op.is_ge, 1.5, Op.add)
+        ts(Fl("tA"), own, 0.0, Op.is_ge, 1.0, Op.add)
+        ts(Fl("tN"), own, 1.0, Op.is_ge, -1.0, Op.add)
+        ts(Fl("tQ"), own, 1.5, Op.is_ge, -1.0, Op.add)
+        tt(W("Q", K, 2 * K), W("o"), W("CB"), Op.subtract)
+        pick(R("e3"), R("gg"))
+        ts(W("SS", K, 2 * K), W("Q", K, 2 * K), -1.0, Op.mult, -float(C), Op.add)
+        oth = ends("e3")
+        ts(W("I"), oth, 1.0, Op.add, 2.0 ** 21, Op.mult)
+        tt(W("vA"), oth, Fl("tA"), Op.is_ge)
+        tt(W("vN"), oth, Fl("tN"), Op.is_lt)
+        ts(W("LH"), W("I"), 1023, Op.bitwise_and)
+        ts(W("LH", K, 2 * K), W("I"), 10, Op.arith_shift_right, 1023, Op.bitwise_and)
+        tt(W("F", K, 2 * K), oth, Fl("tP"), Op.is_ge)
+        tt(W("F"), oth, Fl("tQ"), Op.is_lt)
+        tt(W("F", 2 * K, 3 * K), W("vA"), W("vN"), Op.add)
+        tt(W("D", 0, 44), W("LH", 0, 44), lr, Op.subtract)
+        tt(W("E", K, 2 * K), l, W("LH", K, 2 * K), Op.subtract)
+        fa, fb = W("F", K, 3 * K), W("F", 0, 2 * K)
+        n = [lambda: tt(W("N1", 0, 44), fa, W("Q", 0, 44), Op.mult), lambda: tt(W("N2", 0, 44), fb, W("SS", 0, 44), Op.mult),
+             lambda: tt(W("N3", 0, 44), W("N1", 0, 44), W("N2", 0, 44), Op.add), lambda: tt(W("N4", 0, 44), W("CB", 0, 44), W("N3", 0, 44), Op.add),
+             lambda: cp(U("SL%d" % j, 0, 44), W("N4", 0, 44))]
+        if j == 0:
+            n[0](), n[1]()
+        tt(W("M1", 0, 44), fa, W("D", 0, 44), Op.mult)
+        tt(W("M2", 0, 44), fb, W("E", 0, 44), Op.mult)
+        if j == 0:
+            n[2]()
+        tt(W("M3", 0, 44), W("M1", 0, 44), W("M2", 0, 44), Op.add)
+        if j == 0:
+            n[3]()
+        tt(ln, lr, W("M3", 0, 44), Op.add)
+        if j == 0:
+            n[4]()
+            ts(W("t1"), W("LR1"), float(C), Op.is_ge, -float(C), Op.mult)
+            cp(U("OL1"), W("LR1"))
+            if rd == 0:
+                tt(R("wa", 0, C), R("lrf"), R("wa", 3 * C, 4 * C), Op.subtract)
+                act(R("wa", 2 * C, 3 * C), R("wa", 0, C), scale=F10)
+            tt(R("a1"), R("wa", 0, 2 * C), R("sg1"), Op.add, sl)
+            tt(W("t2"), W("LR1"), W("t1"), Op.add)
+            tt(R("lrs"), R("wa", 2 * C, 4 * C), R("a1"), Op.add, sr)
+            cp(U("OLC1"), W("t2"))
+            return []
+        ts(W("t1", 0, 44), ln, float(C), Op.is_ge, -float(C), Op.mult)
+        cp(U("OL0", 0, 44), ln)
+        tt(W("t2", 0, 44), ln, W("t1", 0, 44), Op.add)
+        cp(R("soR%d" % rd), W("t2", 0, 44))
+        return n
+
+    for rd in range(3):
+        last = rd == 2
+        partner = T.cores[rank ^ STEP[rd]]
+        ra, rb, rc = route(topo, core, partner)
+
+        def to(relay, lo, n):
+            return bits(topo.engines(core, relay)[lo:lo + n])
+
+        def remote(buf, sem, relay, lo, a=0):
+            rid, pid = topo.addr(relay, core)
+            o, i = T["ro%s%d" % (buf, rd)], T["so%s%d" % (buf, rd)]
+            send([R("so%s%d" % (buf, rd))],
+                 lambda: g.remote_dma(o[:], i[:, a:], T.sem["a%s%d" % (sem, rd)], T.sem["ls"], pid, rid, to(relay, lo, 8)), 8)
+
+        signs(0, C if rd == 0 else HALF, 0)
+
+        def more():
+            for t in range(0 if rd == 0 else 4):
+                act(R("win", 704 * t + C, 704 * t + C + HALF), R("ps%d" % (4 + t), 0, HALF), scale=0.5)
+            if rd == 0:
+                replicas(2)
+                ts(R("ri"), R("lrf"), -511.5 * F21, Op.add, 2.0 ** 11, Op.mult)
+                ts(R("wa", C, 2 * C), R("ri"), F21, Op.mult)
+                act(R("wa", 3 * C, 4 * C), R("wa", C, 2 * C), scale=F10)
+            for k in range(2, 4):
+                mm(2 + k, "ur", 128 * k, "qx", "sx", 0, C)
+            act(R("sg1"), R("ps4", 0, C), func=Act.Sign, scale=-1.0)
+            act(R("sgt"), R("ps5", 0, C), func=Act.Sign)
+            act(R("pf1"), R("sgt"), func=Act.Relu, scale=0.5)
+            act(R("pw1", 0, C), R("none"))
+        step(rd, 0, more)
+        slots = step(rd, 1)
+        remote("R", "R", ra, 0, K)
+        for h, (lo, hi) in enumerate(CHUNKS):
+            for t in range(4):
+                if h == 0 and rd == 0:
+                    act(R("win", 704 * t + C, 704 * t + 2 * C), R("lvt", t, 4 * C, 4), scale=0.5)
+            if h == 0:
+                windows()
+            for t in range(4):
+                act(R("gl", C * t + lo, C * t + hi), R("win", 704 * t, 704 * t + 704), U("OL0", lo // 16, hi // 16))
+                tt(R("zt", 4 * lo + t, 4 * hi, 4), R("win", 704 * t, 704 * t + 704), R("gl", C * t + lo, C * t + hi), Op.add, U("OL0", K + lo // 16, K + hi // 16))
+            quant("z", "zt", lo, hi)
+            for b in range(4):
+                mm(4 * h + b, "w", 128 * b, "qz", "sz", lo, hi)
+        for f in slots:
+            f()
+        act(R("wa", 0, C), R("wb"), U("SL1"))
+        if not last:
+            act(R("pw0", 0, C), R("none"))
+        for h, (lo, hi) in enumerate(CHUNKS):
+            for b in range(4):
+                o, i = R("hp", C * b + lo, C * b + hi), R("ps%d" % (4 * h + b), 0, hi - lo)
+                if b % 2 == 0:
+                    ts(o, i, 0.03125, Op.mult)
+                else:
+                    act(o, i, scale=0.03125)
+        arrive("laR%d" % rd, "aR%d" % rd, 8)
+        tt(R("gg"), R("wa", 0, C), R("dm"), Op.mult, R("laR%d" % rd))
+        pick(R("e3"), R("gg"))
+        ts(W("mi"), ends("e3"), 2.0 ** 21, Op.mult)
+        ts(W("mt"), ends("e3"), float(C) * F21, Op.is_ge, -float(C), Op.mult)
+        tt(W("mm"), W("mi"), W("mt"), Op.add)
+        cp(U("MO"), W("mm"))
+        cp(R("soM%d" % rd), W("mm", 11, 22))
+        remote("M", "M", rc, 8)
+        for b in range(4):
+            o, i, n = R("gt", b, 4 * HALF, 4), R("hp", C * b, C * b + C), U("MO", 0, 11)
+            if b % 2 == 0:
+                cp(o, i, n)
+            else:
+                act(o, i, n)
+        q, s = "soQ%d" % rd, "soS%d" % rd
+        quant("", "gt", 0, HALF, q, s)
+
+        def codes():
+            tr = []
+            for relay, lo, e in ((ra, 0, 0), (rb, 88, 8)):
+                rid, pid = topo.addr(relay, core)
+                tr.append(RemoteDMATransfer(dst_ids=[DstId(rid=rid, pnc=pid)], dma_engine_mask=to(relay, e, 8), remote_sem=T.sem["aC%d" % rd],
+                                            src=T[q][:, lo:lo + 88].bitcast(dt.uint8), dst=T["roQ%d" % rd][:, lo:lo + 88].bitcast(dt.uint8)))
+            g.remote_dma_fused(tr, local_sem=T.sem["ls"])
+        send([R(q)], codes, 16)
+        remote("S", "S", rc, 0)
+        act(R("wa", C, 2 * C), R("wb"), U("SL1", K, 2 * K))
+        if rd == 0:
+            quant("e", "et", 0, 512)
+        if not last:
+            act(R("wa", 2 * C, 4 * C), R("wa", 0, 2 * C), scale=F10)
+            parents("pw0", U("OL0"))
+            cp(U("OLC0"), R("soR%d" % rd, 0, K))
+            tt(R("lrf"), R("wa", 0, C), R("wa", 3 * C, 4 * C), Op.add)
+        else:
+            act(R("gro"), R("wa", 0, 2 * C), scale=2.0 ** 21)
+            store("y", T["gr"][:, :], T["gro"][0:128:16, :], R("gro"))
+            quant("v", "vt", 0, 128)
+        arrive("laM%d" % rd, "aM%d" % rd, 8)
+        own = R("laM%d" % rd, 0, 11)
+        for b in range(4):
+            x = R("xt", 4 * HALF + b, 4 * C, 4)
+            tt(x, R("hp", C * b, C * b + C), x, Op.add, own)
+        quant("x", "xt", HALF, C)
+        if not last:
+            signs(HALF, C, 2)
+            for b in range(4):
+                act(R("win", 704 * b + C + HALF, 704 * b + 2 * C), R("hp", C * b, C * b + C), own, scale=0.5)
+        else:
+            mm(0, "v", 0, "qx", "sx", HALF, C)
+            act(R("yo", HALF, C), R("ps0", 0, HALF))
+            store("y", T["oc"][:, 4 * HALF:4 * C], T["qx"][:, HALF:C].bitcast(dt.uint8), R("qx", HALF, C))
+            for k in range(4):
+                store("y", T["osc"][4 * k:4 * k + 4, HALF:C], T["sx"][32 * k:32 * k + 4, HALF:C], R("sx", HALF, C))
+            store("y", T["y"][:, HALF:C], T["yo"][:, HALF:C], R("yo", HALF, C))
+        arrive("laQ%d" % rd, "aC%d" % rd, 16)
+        arrive("laS%d" % rd, "aS%d" % rd, 8)
+        for b in range(4):
+            mm(4 + b, "e", 128 * b, "laQ%d" % rd, "laS%d" % rd, 0, HALF)
+        for b in range(4):
+            x = R("xt", b, 4 * HALF, 4)
+            tt(x, R("ps%d" % (4 + b), 0, HALF), x, Op.add)
+        quant("x", "xt", 0, HALF)
+    mm(1, "v", 0, "qx", "sx", 0, HALF)
+    act(R("yo", 0, HALF), R("ps1", 0, HALF))
+    store("y", T["oc"][:, 0:4 * HALF], T["qx"][:, 0:HALF].bitcast(dt.uint8), R("qx", 0, HALF))
+    for k in range(4):
+        store("s" if k % 2 else "y", T["osc"][4 * k:4 * k + 4, 0:HALF], T["sx"][32 * k:32 * k + 4, 0:HALF], R("sx", 0, HALF))
+    store("s", T["y"][:, 0:HALF], T["yo"][:, 0:HALF], R("yo", 0, HALF))
+    for s in sorted(count):
+        g.wait_ge(T.sem[s], count[s])

@@ -4,12 +4,12 @@ from concourse.mybir import dt, AluOpType, ActivationFunctionType
 Op, Act = AluOpType, ActivationFunctionType
 C, HALF, K = 352, 176, 22
 STEP = [1, 2, 4]
-F21, F10 = 2.0 ** -21, 2.0 ** 10
+FR, F10 = 2.0 ** -22, 2.0 ** 10
 CHUNKS = [(0, 192), (192, 352)]
 WIDE = [("LR0", 44), ("LR1", 44), ("CB", 44), ("F", 66), ("LH", 44), ("D", 44), ("E", 44), ("Q", 44), ("SS", 44), ("M1", 44), ("M2", 44), ("M3", 44),
         ("N1", 44), ("N2", 44), ("N3", 44), ("N4", 44), ("t1", 44), ("t2", 44), ("par", 22), ("x", 22), ("i32", 22), ("A", 22), ("dlp", 22), ("aM", 22),
         ("o", 22), ("I", 22), ("vA", 22), ("vN", 22), ("mi", 22), ("mt", 22), ("mm", 22)]
-U16S = [("OL0", 44), ("OL1", 22), ("OLC0", 22), ("OLC1", 22), ("O", 22), ("SL0", 44), ("SL1", 44), ("LX", 22), ("MO", 22)]
+U16S = [("OLs", 44), ("OL1", 22), ("OLC0", 22), ("OLC1", 22), ("O", 22), ("SL0", 44), ("SL1", 44), ("LX", 22), ("MO", 22)]
 FTHS = [("tA", 22), ("tP", 22), ("tN", 22), ("tQ", 22), ("pk", 22), ("px", 8)]
 
 
@@ -35,12 +35,12 @@ def tiles(kind, **widths):
 
 
 SCRATCH = {
-    **tiles("bfloat16", xt=4 * C, lvt=4 * C, ut=512, vt=512, win=8 * C, gl=4 * C, zt=4 * C, hp=4 * C, gt=4 * HALF, et=2048, one=512),
+    **tiles("bfloat16", xt=4 * C, lvt=4 * C, ut=512, vt=512, win=8 * C, gl=4 * C, zt=4 * C, hp=4 * C, gt=4 * HALF, et=2048, one=512, kmb=C, e1b=C, e2b=C, e1s=C, e2s=C, twb=C, dmb=C),
     **codes_of("x", C), **codes_of("u", 128), **codes_of("ur", 512), **codes_of("v", 128), **codes_of("w", 512), **codes_of("e", 512), **codes_of("z", C),
-    **tiles("int32", lw=K, rw=K, wi=WIN_, ui=32, ri=C),
+    **tiles("int32", lw=K, rw=K, wi=WIN_, ui=32),
     **tiles("uint16", wu=WUN, ux=32),
     **tiles("float32", wf=WFN, ones=32, ex=704, tr=704, kr=C, dm=C, km=C, rc=C, none=C, wa=4 * C, wb=2 * C, lrf=C, lrs=C, a1=C, tw0=2 * C, tw1=2 * C,
-            pw0=2 * C, pw1=2 * C, sg0=C, sg1=C, sgt=C, pf0=C, pf1=C, e1=C, e2=C, gg=C, e3=C, gro=2 * C, yo=C),
+            pw0=2 * C, pw1=2 * C, sg0=C, sg1=C, sgt=C, pf0=C, pf1=2 * C, e1=C, e2=C, gg=C, e3=C, gro=2 * C, yo=C, ll=2 * C),
 }
 for _b in range(8):
     SCRATCH["ps%d" % _b] = ("psum", [128, 512], "float32")
@@ -193,6 +193,9 @@ def rank_program(g, core, T, topo):
         else:
             run("s", lambda: g.scalar.activation(ap(out), src(in_, ind), func, scale=scale), given(in_, ind), [out])
 
+    def shift(out, in_, scale, bias):
+        run("s", lambda: g.scalar.activation(ap(out), ap(in_), Act.Identity, bias=bias, scale=scale), [in_], [out])
+
     def scan(out, d0, d1, op0, op1):
         run("v", lambda: g.vector.tensor_tensor_scan(ap(out), ap(d0), ap(d1), 0.0, op0, op1), [d0, d1], [out])
 
@@ -255,27 +258,29 @@ def rank_program(g, core, T, topo):
     fill(R("ones"), 1.0)
     fill(R("km"), 1.0)
     fill(W("SS"), C)
-    act(R("pw0", 0, C), R("none"))
     ts(W("t1"), W("x"), 31, Op.bitwise_and)
     ts(W("t2"), W("x"), 15, Op.bitwise_and)
     fill(R("km", 0, C, 16), 0.0)
+    act(R("pw0", 0, C), R("none"))
+    act(R("tw0", C, 2 * C), R("none"), scale=0.0)
+    act(R("tw1", C, 2 * C), R("none"), scale=0.0)
+    act(R("kmb"), R("km"))
     cp(Fl("px", 0, 8), W("t2", 0, 8))
     tt(W("mt"), W("t1"), W("i32"), Op.add)
     px = Fl("px", 0, 1)
     run("v", lambda: g.vector.tensor_scalar(T["dm"][:], T["kr"][:], ap(px), None, Op.is_equal), [R("kr"), px], [R("dm")])
+    act(R("dmb"), R("dm"))
     cp(U("LX"), W("mt"))
     tt(W("CB"), W("t2"), W("mm"), Op.add)
     cp(R("ux"), R("ui"))
     ts(W("CB", K, 2 * K), W("CB"), float(C), Op.add)
 
     ts(W("mi"), R("rw"), 1024.0, Op.mult)
-    cp(U("OL0"), R("lw"))
+    cp(U("OLs"), R("lw"))
     tt(Fl("pk"), W("mi"), R("lw"), Op.add)
     for q in range(K):
         o, i = R("ex", 32 * q, 32 * q + 32), Fl("pk", q, q + 1)
         run("s", lambda: g.scalar.activation(ap(o), T["ones"][:], Act.Copy, scale=ap(i)), [R("ones"), i], [o])
-    fill(R("tw0", C, 2 * C), 0.0)
-    quant("u", "ut", 0, 128)
 
     def replicas(k):
         a, e = 128 * k, 8 * k
@@ -284,22 +289,30 @@ def rank_program(g, core, T, topo):
         run("s", lambda: g.scalar.activation(T["sur"][:, a:a + 256], T["su"][:, 0:128].indirect(T["ux"][:, e:e + 16]), Act.Copy),
             [R("su"), R("ux")], [R("sur", a, a + 256)])
 
-    def parents(pw, ol):
+    def parents(pw, ol, *between):
+        f = list(between) + [lambda: None] * 2
         put(R(pw), ol, R("rc"))
+        f[0]()
         masked(R("e1"), R(pw, 0, C))
+        f[1]()
         pick(R("e2"), R("e1"))
         cp(W("par"), ends("e2"))
 
-    replicas(0)
+    def start():
+        quant("u", "ut", 0, 128)
+        replicas(0)
+
+    lists = [U("OLs"), None]
+    parents("pw0", lists[0], start)
     run("v", lambda: g.vector.transpose(T["tr"][:], T["ex"][:]), [R("ex")], [R("tr")])
-    act(R("lrf"), R("tr"), U("LX"), scale=F21)
-    fill(R("one"), 1.0)
+    act(R("lrf"), R("tr"), U("LX"), scale=FR)
+    shift(R("one", 0, C), R("none"), 0.0, 1.0)
+    shift(R("one", C, 512), R("none", 0, 160), 0.0, 1.0)
     cp(W("LR0"), R("lw"))
     cp(W("LR0", K, 2 * K), R("rw"))
     col16(U("OLC0"), W("LR0"))
+    tt(W("dlp"), W("LR0"), W("par"), Op.subtract)
     quant("x", "xt", 0, C)
-    parents("pw0", U("OL0"))
-    fill(R("tw1", C, 2 * C), 0.0)
     for b in range(4):
         run("p", lambda: g.affine_select(T["et"][:, 512 * b:512 * b + 512], T["one"][:], [[-1, 512]], Op.is_equal, 0.0, b, 4),
             [R("one")], [R("et", 512 * b, 512 * b + 512)])
@@ -308,46 +321,66 @@ def rank_program(g, core, T, topo):
         for t in range(4):
             act(R("win", 704 * t, 704 * t + C), R("xt", t, 4 * C, 4), scale=0.5)
 
-    def signs(lo, hi, bank):
+    def scores(lo, hi, bank):
         for k in range(2):
             mm(bank + k, "ur", 128 * k, "qx", "sx", lo, hi)
         act(R("sg0", lo, hi), R("ps%d" % bank, 0, hi - lo), func=Act.Sign, scale=-1.0)
+
+    def signs(lo, hi, bank):
         ts(R("pf0", lo, hi), R("ps%d" % (bank + 1), 0, hi - lo), 0.0, Op.is_gt, 0.5, Op.mult)
+        scan(R("e1s", lo, hi), R("ps%d" % bank, 0, hi - lo), R("dm", lo, hi), Op.add, Op.mult)
         tt(R("lrs", lo, hi), R("lrf", lo, hi), R("sg0", lo, hi), Op.add)
+        scan(R("e2s", lo, hi), R("kmb", lo, hi), R("e1s", lo, hi), Op.mult, Op.add)
+        ts(W("A", lo // 16, hi // 16), ("e2s", lo + 15, hi, 16), 0.0, Op.is_gt)
 
     def step(rd, j, more=None):
         lr, ln = W("LR%d" % j, 0, 44), W("LR%d" % (1 - j), 0, 44)
         l, r = W("LR%d" % j), W("LR%d" % j, K, 2 * K)
-        olc, tw, pf = U("OLC%d" % j), "tw%d" % j, R("pf%d" % j)
+        tw, pf = "tw%d" % j, R("pf%d" % j)
         sl, sr = U("SL0", 0, K), U("SL0", K, 2 * K)
         if j == 0:
-            tt(R(tw, 0, C), pf, R("lrs"), Op.add, olc)
+            tt(R(tw, 0, C), pf, R("lrs"), Op.add, U("OLC0"))
+            act(R("twb"), R(tw, 0, C))
             more()
         else:
-            tt(R(tw, 0, C), pf, R("lrs"), Op.add, olc)
+            tt(R(tw, 0, C), pf, R("lrs"), Op.add, U("OL1"))
+            act(R("twb"), R(tw, 0, C))
             act(R("wb", 0, C), R("wa", 0, 2 * C), sl)
             act(R("wb", C, 2 * C), R("wa", 0, 2 * C), sr)
-            parents("pw1", U("OL1"))
-        masked(R("e1"), R(tw, 0, C))
-        tt(W("dlp"), l, W("par"), Op.subtract)
+        own = ends("e2b")
+
+        def ownmask():
+            scan(R("e1b"), R("twb"), R("dmb"), Op.add, Op.mult)
+
+        def picked():
+            scan(R("e2b"), R("kmb"), R("e1b"), Op.mult, Op.add)
+
+        if j == 1:
+            parents("pw1", U("OL1"), ownmask, picked)
+            ts(W("A"), own, 0.0, Op.is_lt)
+            tt(W("dlp"), l, W("par"), Op.subtract)
         tt(W("E"), r, l, Op.subtract)
-        tt(W("Q"), l, W("CB"), Op.subtract)
-        pick(R("e2"), R("e1"))
-        own = ends("e2")
-        ts(W("A"), own, 0.0, Op.is_lt)
         tt(W("aM"), W("A"), W("dlp"), Op.mult)
+        tt(W("Q"), l, W("CB"), Op.subtract)
         tt(W("o"), W("aM"), W("par"), Op.add)
         cp(U("O"), W("o"))
         tt(R("gg"), R(tw), R("dm"), Op.mult, U("O"))
+        tt(W("Q", K, 2 * K), W("o"), W("CB"), Op.subtract)
+        oth = ends("e3")
+        if j == 0:
+            ownmask()
+            pick(R("e3"), R("gg"))
+            picked()
+            ts(W("I"), oth, 1.0, Op.add, 2.0 ** 22, Op.mult)
         ts(Fl("tP"), own, 0.0, Op.is_ge, 1.5, Op.add)
         ts(Fl("tA"), own, 0.0, Op.is_ge, 1.0, Op.add)
         ts(Fl("tN"), own, 1.0, Op.is_ge, -1.0, Op.add)
         ts(Fl("tQ"), own, 1.5, Op.is_ge, -1.0, Op.add)
-        tt(W("Q", K, 2 * K), W("o"), W("CB"), Op.subtract)
-        pick(R("e3"), R("gg"))
+        if j == 1:
+            pick(R("e3"), R("gg"))
         ts(W("SS", K, 2 * K), W("Q", K, 2 * K), -1.0, Op.mult, -float(C), Op.add)
-        oth = ends("e3")
-        ts(W("I"), oth, 1.0, Op.add, 2.0 ** 21, Op.mult)
+        if j == 1:
+            ts(W("I"), oth, 1.0, Op.add, 2.0 ** 22, Op.mult)
         tt(W("vA"), oth, Fl("tA"), Op.is_ge)
         tt(W("vN"), oth, Fl("tN"), Op.is_lt)
         ts(W("LH"), W("I"), 1023, Op.bitwise_and)
@@ -365,29 +398,23 @@ def rank_program(g, core, T, topo):
             n[0](), n[1]()
         tt(W("M1", 0, 44), fa, W("D", 0, 44), Op.mult)
         tt(W("M2", 0, 44), fb, W("E", 0, 44), Op.mult)
-        if j == 0:
-            n[2]()
+        n[2 if j == 0 else 0]()
         tt(W("M3", 0, 44), W("M1", 0, 44), W("M2", 0, 44), Op.add)
-        if j == 0:
-            n[3]()
+        n[3 if j == 0 else 1]()
         tt(ln, lr, W("M3", 0, 44), Op.add)
         if j == 0:
             n[4]()
-            ts(W("t1"), W("LR1"), float(C), Op.is_ge, -float(C), Op.mult)
             cp(U("OL1"), W("LR1"))
             if rd == 0:
                 tt(R("wa", 0, C), R("lrf"), R("wa", 3 * C, 4 * C), Op.subtract)
                 act(R("wa", 2 * C, 3 * C), R("wa", 0, C), scale=F10)
             tt(R("a1"), R("wa", 0, 2 * C), R("sg1"), Op.add, sl)
-            tt(W("t2"), W("LR1"), W("t1"), Op.add)
             tt(R("lrs"), R("wa", 2 * C, 4 * C), R("a1"), Op.add, sr)
-            cp(U("OLC1"), W("t2"))
-            return []
-        ts(W("t1", 0, 44), ln, float(C), Op.is_ge, -float(C), Op.mult)
-        cp(U("OL0", 0, 44), ln)
-        tt(W("t2", 0, 44), ln, W("t1", 0, 44), Op.add)
-        cp(R("soR%d" % rd), W("t2", 0, 44))
-        return n
+        else:
+            n[2]()
+            cp(R("soR%d" % rd), ln)
+            n[3]()
+            n[4]()
 
     for rd in range(3):
         last = rd == 2
@@ -403,6 +430,9 @@ def rank_program(g, core, T, topo):
             send([R("so%s%d" % (buf, rd))],
                  lambda: g.remote_dma(o[:], i[:, a:], T.sem["a%s%d" % (sem, rd)], T.sem["ls"], pid, rid, to(relay, lo, 8)), 8)
 
+        scores(0, C if rd == 0 else HALF, 0)
+        if rd > 0:
+            signs(HALF, C, 2)
         signs(0, C if rd == 0 else HALF, 0)
 
         def more():
@@ -410,18 +440,23 @@ def rank_program(g, core, T, topo):
                 act(R("win", 704 * t + C, 704 * t + C + HALF), R("ps%d" % (4 + t), 0, HALF), scale=0.5)
             if rd == 0:
                 replicas(2)
-                ts(R("ri"), R("lrf"), -511.5 * F21, Op.add, 2.0 ** 11, Op.mult)
-                ts(R("wa", C, 2 * C), R("ri"), F21, Op.mult)
-                act(R("wa", 3 * C, 4 * C), R("wa", C, 2 * C), scale=F10)
+                shift(R("sgt"), R("lrf"), 2.0 ** 12, -511.0 / 1024)
+                shift(R("a1"), R("sgt"), 1.0, 1.5 * 2.0 ** 23)
+                shift(R("sg1"), R("a1"), 1.0, -1.5 * 2.0 ** 23)
+                act(R("wa", 3 * C, 4 * C), R("sg1"), scale=FR * F10)
+                act(R("wa", C, 2 * C), R("sg1"), scale=FR)
             for k in range(2, 4):
                 mm(2 + k, "ur", 128 * k, "qx", "sx", 0, C)
             act(R("sg1"), R("ps4", 0, C), func=Act.Sign, scale=-1.0)
             act(R("sgt"), R("ps5", 0, C), func=Act.Sign)
-            act(R("pf1"), R("sgt"), func=Act.Relu, scale=0.5)
+            act(R("pf1", 0, C), R("sgt"), func=Act.Relu, scale=0.5)
+            act(R("pf1", C, 2 * C), R("sgt"), func=Act.Relu, scale=0.5)
             act(R("pw1", 0, C), R("none"))
         step(rd, 0, more)
-        slots = step(rd, 1)
+        step(rd, 1)
         remote("R", "R", ra, 0, K)
+        lists[0], lists[1] = R("soR%d" % rd, 0, K), R("soR%d" % rd, K, 2 * K)
+        part = lambda r, lo, hi: (r[0], r[1] + lo // 16, r[1] + hi // 16, 1)
         for h, (lo, hi) in enumerate(CHUNKS):
             for t in range(4):
                 if h == 0 and rd == 0:
@@ -429,16 +464,11 @@ def rank_program(g, core, T, topo):
             if h == 0:
                 windows()
             for t in range(4):
-                act(R("gl", C * t + lo, C * t + hi), R("win", 704 * t, 704 * t + 704), U("OL0", lo // 16, hi // 16))
-                tt(R("zt", 4 * lo + t, 4 * hi, 4), R("win", 704 * t, 704 * t + 704), R("gl", C * t + lo, C * t + hi), Op.add, U("OL0", K + lo // 16, K + hi // 16))
+                act(R("gl", C * t + lo, C * t + hi), R("win", 704 * t, 704 * t + 704), part(lists[0], lo, hi))
+                tt(R("zt", 4 * lo + t, 4 * hi, 4), R("win", 704 * t, 704 * t + 704), R("gl", C * t + lo, C * t + hi), Op.add, part(lists[1], lo, hi))
             quant("z", "zt", lo, hi)
             for b in range(4):
                 mm(4 * h + b, "w", 128 * b, "qz", "sz", lo, hi)
-        for f in slots:
-            f()
-        act(R("wa", 0, C), R("wb"), U("SL1"))
-        if not last:
-            act(R("pw0", 0, C), R("none"))
         for h, (lo, hi) in enumerate(CHUNKS):
             for b in range(4):
                 o, i = R("hp", C * b + lo, C * b + hi), R("ps%d" % (4 * h + b), 0, hi - lo)
@@ -446,11 +476,14 @@ def rank_program(g, core, T, topo):
                     ts(o, i, 0.03125, Op.mult)
                 else:
                     act(o, i, scale=0.03125)
+            if h == 0:
+                act(R("ll", 0, C), R("wb"), U("SL1", 0, K))
+                act(R("ll", C, 2 * C), R("ll", 0, C))
         arrive("laR%d" % rd, "aR%d" % rd, 8)
-        tt(R("gg"), R("wa", 0, C), R("dm"), Op.mult, R("laR%d" % rd))
+        tt(R("gg"), R("ll"), R("dm"), Op.mult, R("laR%d" % rd))
         pick(R("e3"), R("gg"))
-        ts(W("mi"), ends("e3"), 2.0 ** 21, Op.mult)
-        ts(W("mt"), ends("e3"), float(C) * F21, Op.is_ge, -float(C), Op.mult)
+        ts(W("mi"), ends("e3"), 2.0 ** 22, Op.mult)
+        ts(W("mt"), ends("e3"), float(C) * FR, Op.is_ge, -float(C), Op.mult)
         tt(W("mm"), W("mi"), W("mt"), Op.add)
         cp(U("MO"), W("mm"))
         cp(R("soM%d" % rd), W("mm", 11, 22))
@@ -473,16 +506,21 @@ def rank_program(g, core, T, topo):
             g.remote_dma_fused(tr, local_sem=T.sem["ls"])
         send([R(q)], codes, 16)
         remote("S", "S", rc, 0)
+        if not last:
+            act(R("pw0", 0, C), R("none"))
         act(R("wa", C, 2 * C), R("wb"), U("SL1", K, 2 * K))
+        act(R("wa", 0, C), R("ll", 0, C))
+        if not last:
+            act(R("wa", 2 * C, 4 * C), R("wa", 0, 2 * C), scale=F10)
+            parents("pw0", lists[0])
+            col16(U("OLC0"), W("LR0"))
+            tt(W("dlp"), W("LR0"), W("par"), Op.subtract)
         if rd == 0:
             quant("e", "et", 0, 512)
         if not last:
-            act(R("wa", 2 * C, 4 * C), R("wa", 0, 2 * C), scale=F10)
-            parents("pw0", U("OL0"))
-            cp(U("OLC0"), R("soR%d" % rd, 0, K))
             tt(R("lrf"), R("wa", 0, C), R("wa", 3 * C, 4 * C), Op.add)
         else:
-            act(R("gro"), R("wa", 0, 2 * C), scale=2.0 ** 21)
+            act(R("gro"), R("wa", 0, 2 * C), scale=2.0 ** 22)
             store("y", T["gr"][:, :], T["gro"][0:128:16, :], R("gro"))
             quant("v", "vt", 0, 128)
         arrive("laM%d" % rd, "aM%d" % rd, 8)
@@ -492,7 +530,6 @@ def rank_program(g, core, T, topo):
             tt(x, R("hp", C * b, C * b + C), x, Op.add, own)
         quant("x", "xt", HALF, C)
         if not last:
-            signs(HALF, C, 2)
             for b in range(4):
                 act(R("win", 704 * b + C + HALF, 704 * b + 2 * C), R("hp", C * b, C * b + C), own, scale=0.5)
         else:
@@ -506,6 +543,8 @@ def rank_program(g, core, T, topo):
         arrive("laS%d" % rd, "aS%d" % rd, 8)
         for b in range(4):
             mm(4 + b, "e", 128 * b, "laQ%d" % rd, "laS%d" % rd, 0, HALF)
+        if not last:
+            scores(HALF, C, 2)
         for b in range(4):
             x = R("xt", b, 4 * HALF, 4)
             tt(x, R("ps%d" % (4 + b), 0, HALF), x, Op.add)

@@ -8,7 +8,7 @@ FR, F10 = 2.0 ** -22, 2.0 ** 10
 CHUNKS = [(0, 192), (192, 352)]
 WIDE = [("LR0", 44), ("LR1", 44), ("CB", 44), ("F", 66), ("LH", 44), ("D", 44), ("E", 44), ("Q", 44), ("SS", 44), ("M1", 44), ("M2", 44), ("M3", 44),
         ("N1", 44), ("N2", 44), ("N3", 44), ("N4", 44), ("t1", 44), ("t2", 44), ("par", 22), ("x", 22), ("i32", 22), ("A", 22), ("dlp", 22), ("aM", 22),
-        ("o", 22), ("I", 22), ("vA", 22), ("vN", 22), ("mi", 22), ("mt", 22), ("mm", 22)]
+        ("o", 22), ("I", 22), ("vA", 22), ("vN", 22), ("mi", 22), ("mt", 22), ("mm", 22), ("c704", 22)]
 U16S = [("OLs", 44), ("OL1", 22), ("OLC0", 22), ("OLC1", 22), ("O", 22), ("SL0", 44), ("SL1", 44), ("LX", 22), ("MO", 22)]
 FTHS = [("tA", 22), ("tP", 22), ("tN", 22), ("tQ", 22), ("pk", 22), ("px", 8)]
 
@@ -39,8 +39,8 @@ SCRATCH = {
     **codes_of("x", C), **codes_of("u", 128), **codes_of("ur", 512), **codes_of("v", 128), **codes_of("w", 512), **codes_of("e", 512), **codes_of("z", C),
     **tiles("int32", lw=K, rw=K, wi=WIN_, ui=32),
     **tiles("uint16", wu=WUN, ux=32),
-    **tiles("float32", wf=WFN, ones=32, ex=704, tr=704, kr=C, dm=C, km=C, rc=C, none=C, wa=4 * C, wb=2 * C, lrf=C, lrs=C, a1=C, tw0=2 * C, tw1=2 * C,
-            pw0=2 * C, pw1=2 * C, sg0=C, sg1=C, sgt=C, pf0=C, pf1=2 * C, e1=C, e2=C, gg=C, e3=C, gro=2 * C, yo=C, ll=2 * C),
+    **tiles("float32", wf=WFN, ones=32, ex=704, tr=704, kr=C, dm=C, km=C, rc=C, none=C, wa=4 * C, wb=4 * C, lrf=C, lrs=C, a1=C, tw0=2 * C, tw1=4 * C,
+            pw0=2 * C, sg0=C, sg1=C, sgt=C, pf0=C, pf1=2 * C, e1=C, e2=C, gg=C, e3=C, gro=2 * C, yo=C, ll=2 * C),
 }
 for _b in range(8):
     SCRATCH["ps%d" % _b] = ("psum", [128, 512], "float32")
@@ -66,6 +66,10 @@ def bits(engines):
     return sum(1 << e for e in engines)
 
 
+def sent_on(kind, rd):
+    return 16 if kind == "S" or (kind == "R" and rd) else 8
+
+
 def relay_program(g, core, T, topo, rank):
     src, sent = T.cores[rank], 0
     for rd, s in enumerate(STEP):
@@ -77,7 +81,7 @@ def relay_program(g, core, T, topo, rank):
         eng = topo.engines(core, dst)[:8]
         jobs = {a: [("R", "R", 0, K), ("C", "Q", 0, 88)], b: [("C", "Q", 88, HALF)], c: [("M", "M", 0, 11), ("S", "S", 0, HALF)]}[core]
         for sem, buf, lo, hi in jobs:
-            g.wait_ge(T.sem["a%s%d" % (sem, rd)], 8)
+            g.wait_ge(T.sem["a%s%d" % (sem, rd)], sent_on(sem, rd))
             o, i = T["la%s%d" % (buf, rd)][:, lo:hi], T["ro%s%d" % (buf, rd)][:, lo:hi]
             if buf == "Q":
                 o, i = o.bitcast(dt.uint8), i.bitcast(dt.uint8)
@@ -265,15 +269,19 @@ def rank_program(g, core, T, topo):
     act(R("tw0", C, 2 * C), R("none"), scale=0.0)
     act(R("tw1", C, 2 * C), R("none"), scale=0.0)
     act(R("kmb"), R("km"))
+    act(R("wb", 2 * C, 3 * C), R("none"), scale=0.0)
     cp(Fl("px", 0, 8), W("t2", 0, 8))
     tt(W("mt"), W("t1"), W("i32"), Op.add)
     px = Fl("px", 0, 1)
+    shift(R("one", 0, C), R("none"), 0.0, 1.0)
+    shift(R("one", C, 512), R("none", 0, 160), 0.0, 1.0)
     run("v", lambda: g.vector.tensor_scalar(T["dm"][:], T["kr"][:], ap(px), None, Op.is_equal), [R("kr"), px], [R("dm")])
     act(R("dmb"), R("dm"))
     cp(U("LX"), W("mt"))
     tt(W("CB"), W("t2"), W("mm"), Op.add)
     cp(R("ux"), R("ui"))
     ts(W("CB", K, 2 * K), W("CB"), float(C), Op.add)
+    ts(W("c704"), W("CB"), 2.0 * C, Op.add)
 
     ts(W("mi"), R("rw"), 1024.0, Op.mult)
     cp(U("OLs"), R("lw"))
@@ -304,15 +312,13 @@ def rank_program(g, core, T, topo):
 
     lists = [U("OLs"), None]
     parents("pw0", lists[0], start)
+    quant("x", "xt", 0, C)
     run("v", lambda: g.vector.transpose(T["tr"][:], T["ex"][:]), [R("ex")], [R("tr")])
     act(R("lrf"), R("tr"), U("LX"), scale=FR)
-    shift(R("one", 0, C), R("none"), 0.0, 1.0)
-    shift(R("one", C, 512), R("none", 0, 160), 0.0, 1.0)
     cp(W("LR0"), R("lw"))
     cp(W("LR0", K, 2 * K), R("rw"))
     col16(U("OLC0"), W("LR0"))
     tt(W("dlp"), W("LR0"), W("par"), Op.subtract)
-    quant("x", "xt", 0, C)
     for b in range(4):
         run("p", lambda: g.affine_select(T["et"][:, 512 * b:512 * b + 512], T["one"][:], [[-1, 512]], Op.is_equal, 0.0, b, 4),
             [R("one")], [R("et", 512 * b, 512 * b + 512)])
@@ -333,7 +339,7 @@ def rank_program(g, core, T, topo):
         scan(R("e2s", lo, hi), R("kmb", lo, hi), R("e1s", lo, hi), Op.mult, Op.add)
         ts(W("A", lo // 16, hi // 16), ("e2s", lo + 15, hi, 16), 0.0, Op.is_gt)
 
-    def step(rd, j, more=None):
+    def step(rd, j, more=None, rest=None):
         lr, ln = W("LR%d" % j, 0, 44), W("LR%d" % (1 - j), 0, 44)
         l, r = W("LR%d" % j), W("LR%d" % j, K, 2 * K)
         tw, pf = "tw%d" % j, R("pf%d" % j)
@@ -356,15 +362,22 @@ def rank_program(g, core, T, topo):
             scan(R("e2b"), R("kmb"), R("e1b"), Op.mult, Op.add)
 
         if j == 1:
-            parents("pw1", U("OL1"), ownmask, picked)
+            put(R(tw, 2 * C, 4 * C), U("OL1"), R("a1"))
+            shift(R("wb", 3 * C, 4 * C), R(tw, 2 * C, 3 * C), 1.0 / F10, 1.0 / F10)
+            ownmask()
+            tt(W("dlp"), l, W("c704"), Op.subtract)
+            picked()
+            tt(W("E"), r, l, Op.subtract)
             ts(W("A"), own, 0.0, Op.is_lt)
-            tt(W("dlp"), l, W("par"), Op.subtract)
-        tt(W("E"), r, l, Op.subtract)
+            tt(W("Q"), l, W("CB"), Op.subtract)
         tt(W("aM"), W("A"), W("dlp"), Op.mult)
-        tt(W("Q"), l, W("CB"), Op.subtract)
-        tt(W("o"), W("aM"), W("par"), Op.add)
+        if j == 0:
+            tt(W("E"), r, l, Op.subtract)
+        tt(W("o"), W("aM"), W("par") if j == 0 else W("c704"), Op.add)
+        if j == 0:
+            tt(W("Q"), l, W("CB"), Op.subtract)
         cp(U("O"), W("o"))
-        tt(R("gg"), R(tw), R("dm"), Op.mult, U("O"))
+        tt(R("gg"), R(tw, 0, (2 if j == 0 else 3) * C), R("dm"), Op.mult, U("O"))
         tt(W("Q", K, 2 * K), W("o"), W("CB"), Op.subtract)
         oth = ends("e3")
         if j == 0:
@@ -376,7 +389,12 @@ def rank_program(g, core, T, topo):
         ts(Fl("tA"), own, 0.0, Op.is_ge, 1.0, Op.add)
         ts(Fl("tN"), own, 1.0, Op.is_ge, -1.0, Op.add)
         ts(Fl("tQ"), own, 1.5, Op.is_ge, -1.0, Op.add)
-        if j == 1:
+        if j == 0:
+            if rd == 0:
+                tt(R("wa", 0, C), R("lrf"), R("wa", 3 * C, 4 * C), Op.subtract)
+                act(R("wa", 2 * C, 3 * C), R("wa", 0, C), scale=F10)
+            rest()
+        else:
             pick(R("e3"), R("gg"))
         ts(W("SS", K, 2 * K), W("Q", K, 2 * K), -1.0, Op.mult, -float(C), Op.add)
         if j == 1:
@@ -405,11 +423,8 @@ def rank_program(g, core, T, topo):
         if j == 0:
             n[4]()
             cp(U("OL1"), W("LR1"))
-            if rd == 0:
-                tt(R("wa", 0, C), R("lrf"), R("wa", 3 * C, 4 * C), Op.subtract)
-                act(R("wa", 2 * C, 3 * C), R("wa", 0, C), scale=F10)
-            tt(R("a1"), R("wa", 0, 2 * C), R("sg1"), Op.add, sl)
-            tt(R("lrs"), R("wa", 2 * C, 4 * C), R("a1"), Op.add, sr)
+            tt(R("a1"), R("wa", 2 * C, 4 * C), R("sg1"), Op.add, sr)
+            tt(R("lrs"), R("wa", 0, 2 * C), R("a1"), Op.add, sl)
         else:
             n[2]()
             cp(R("soR%d" % rd), ln)
@@ -424,11 +439,11 @@ def rank_program(g, core, T, topo):
         def to(relay, lo, n):
             return bits(topo.engines(core, relay)[lo:lo + n])
 
-        def remote(buf, sem, relay, lo, a=0):
+        def remote(buf, sem, relay, lo, n, a=0):
             rid, pid = topo.addr(relay, core)
             o, i = T["ro%s%d" % (buf, rd)], T["so%s%d" % (buf, rd)]
             send([R("so%s%d" % (buf, rd))],
-                 lambda: g.remote_dma(o[:], i[:, a:], T.sem["a%s%d" % (sem, rd)], T.sem["ls"], pid, rid, to(relay, lo, 8)), 8)
+                 lambda: g.remote_dma(o[:], i[:, a:], T.sem["a%s%d" % (sem, rd)], T.sem["ls"], pid, rid, to(relay, lo, n)), n)
 
         scores(0, C if rd == 0 else HALF, 0)
         if rd > 0:
@@ -439,22 +454,26 @@ def rank_program(g, core, T, topo):
             for t in range(0 if rd == 0 else 4):
                 act(R("win", 704 * t + C, 704 * t + C + HALF), R("ps%d" % (4 + t), 0, HALF), scale=0.5)
             if rd == 0:
-                replicas(2)
                 shift(R("sgt"), R("lrf"), 2.0 ** 12, -511.0 / 1024)
                 shift(R("a1"), R("sgt"), 1.0, 1.5 * 2.0 ** 23)
                 shift(R("sg1"), R("a1"), 1.0, -1.5 * 2.0 ** 23)
                 act(R("wa", 3 * C, 4 * C), R("sg1"), scale=FR * F10)
                 act(R("wa", C, 2 * C), R("sg1"), scale=FR)
+                replicas(2)
             for k in range(2, 4):
                 mm(2 + k, "ur", 128 * k, "qx", "sx", 0, C)
             act(R("sg1"), R("ps4", 0, C), func=Act.Sign, scale=-1.0)
+
+        def rest():
             act(R("sgt"), R("ps5", 0, C), func=Act.Sign)
             act(R("pf1", 0, C), R("sgt"), func=Act.Relu, scale=0.5)
             act(R("pf1", C, 2 * C), R("sgt"), func=Act.Relu, scale=0.5)
-            act(R("pw1", 0, C), R("none"))
-        step(rd, 0, more)
+            act(R("tw1", 2 * C, 3 * C), R("none"), scale=0.0)
+            if not last:
+                act(R("pw0", 0, C), R("none"))
+        step(rd, 0, more, rest)
         step(rd, 1)
-        remote("R", "R", ra, 0, K)
+        remote("R", "R", ra, 0, sent_on("R", rd), K)
         lists[0], lists[1] = R("soR%d" % rd, 0, K), R("soR%d" % rd, K, 2 * K)
         part = lambda r, lo, hi: (r[0], r[1] + lo // 16, r[1] + hi // 16, 1)
         for h, (lo, hi) in enumerate(CHUNKS):
@@ -469,15 +488,15 @@ def rank_program(g, core, T, topo):
             quant("z", "zt", lo, hi)
             for b in range(4):
                 mm(4 * h + b, "w", 128 * b, "qz", "sz", lo, hi)
+        act(R("ll", 0, C), R("wb", 0, 2 * C), U("SL1", 0, K))
         for h, (lo, hi) in enumerate(CHUNKS):
             for b in range(4):
                 o, i = R("hp", C * b + lo, C * b + hi), R("ps%d" % (4 * h + b), 0, hi - lo)
-                if b % 2 == 0:
+                if b % 2 == 0 or (h, b) == (1, 3):
                     ts(o, i, 0.03125, Op.mult)
                 else:
                     act(o, i, scale=0.03125)
             if h == 0:
-                act(R("ll", 0, C), R("wb"), U("SL1", 0, K))
                 act(R("ll", C, 2 * C), R("ll", 0, C))
         arrive("laR%d" % rd, "aR%d" % rd, 8)
         tt(R("gg"), R("ll"), R("dm"), Op.mult, R("laR%d" % rd))
@@ -487,7 +506,7 @@ def rank_program(g, core, T, topo):
         tt(W("mm"), W("mi"), W("mt"), Op.add)
         cp(U("MO"), W("mm"))
         cp(R("soM%d" % rd), W("mm", 11, 22))
-        remote("M", "M", rc, 8)
+        remote("M", "M", rc, 8, sent_on("M", rd))
         for b in range(4):
             o, i, n = R("gt", b, 4 * HALF, 4), R("hp", C * b, C * b + C), U("MO", 0, 11)
             if b % 2 == 0:
@@ -505,15 +524,14 @@ def rank_program(g, core, T, topo):
                                             src=T[q][:, lo:lo + 88].bitcast(dt.uint8), dst=T["roQ%d" % rd][:, lo:lo + 88].bitcast(dt.uint8)))
             g.remote_dma_fused(tr, local_sem=T.sem["ls"])
         send([R(q)], codes, 16)
-        remote("S", "S", rc, 0)
-        if not last:
-            act(R("pw0", 0, C), R("none"))
+        remote("S", "S", rc, 0, sent_on("S", rd))
         act(R("wa", C, 2 * C), R("wb"), U("SL1", K, 2 * K))
         act(R("wa", 0, C), R("ll", 0, C))
         if not last:
             act(R("wa", 2 * C, 4 * C), R("wa", 0, 2 * C), scale=F10)
-            parents("pw0", lists[0])
-            col16(U("OLC0"), W("LR0"))
+            parents("pw0", lists[0], lambda: ts(W("t1"), W("LR0"), float(C), Op.is_ge, -float(C), Op.mult),
+                    lambda: tt(W("t2"), W("LR0"), W("t1"), Op.add))
+            cp(U("OLC0"), W("t2"))
             tt(W("dlp"), W("LR0"), W("par"), Op.subtract)
         if rd == 0:
             quant("e", "et", 0, 512)

from concourse.bass import DstId, RemoteDMATransfer
from concourse.mybir import dt, AluOpType, ActivationFunctionType

Op, Act = AluOpType, ActivationFunctionType
C, HALF, K = 352, 176, 22
STEP = [1, 2, 4]
FR, F10 = 2.0 ** -22, 2.0 ** 10
CHUNKS = [(0, 192), (192, 352)]
WIDE = [("LR0", 44), ("LR1", 44), ("CB", 44), ("F", 66), ("LH", 44), ("D", 44), ("E", 44), ("Q", 44), ("SS", 44), ("M1", 44), ("M2", 44), ("M3", 44),
        ("N1", 44), ("N2", 44), ("N3", 44), ("N4", 44), ("t1", 44), ("t2", 44), ("par", 22), ("x", 22), ("i32", 22), ("A", 22), ("dlp", 22), ("aM", 22),
        ("o", 22), ("I", 22), ("vA", 22), ("vN", 22), ("mi", 22), ("mt", 22), ("mm", 22), ("c704", 22)]
U16S = [("OLs", 44), ("OL1", 22), ("OLC0", 22), ("OLC1", 22), ("O", 22), ("SL0", 44), ("SL1", 44), ("LX", 22), ("MO", 22)]
FTHS = [("tA", 22), ("tP", 22), ("tN", 22), ("tQ", 22), ("pk", 22), ("px", 8)]


def places(blocks):
    at, d = 0, {}
    for n, w in blocks:
        d[n] = at
        at += (w + 7) // 8 * 8
    return d, at


WI, WIN_ = places(WIDE)
WU, WUN = places(U16S)
WF, WFN = places(FTHS)


def codes_of(name, n):
    return {"q" + name: ("sbuf", [128, n], "float8_e4m3fn_x4"), "s" + name: ("sbuf", [128, n], "uint8")}


def tiles(kind, **widths):
    return {k: ("sbuf", [128, w], kind) for k, w in widths.items()}


SCRATCH = {
    **tiles("bfloat16", xt=4 * C, lvt=4 * C, ut=512, vt=512, win=8 * C, gl=4 * C, zt=4 * C, hp=4 * C, gt=4 * HALF, et=2048, one=512, kmb=C, e1b=C, e2b=C, e1s=C, e2s=C, twb=C, dmb=C),
    **codes_of("x", C), **codes_of("u", 128), **codes_of("ur", 512), **codes_of("v", 128), **codes_of("w", 512), **codes_of("e", 512), **codes_of("z", C),
    **tiles("int32", lw=K, rw=K, wi=WIN_, ui=32),
    **tiles("uint16", wu=WUN, ux=32),
    **tiles("float32", wf=WFN, ones=32, ex=704, tr=704, kr=C, dm=C, km=C, rc=C, none=C, wa=4 * C, wb=4 * C, lrf=C, lrs=C, a1=C, tw0=2 * C, tw1=4 * C,
            pw0=2 * C, sg0=C, sg1=C, sgt=C, pf0=C, pf1=2 * C, e1=C, e2=C, gg=C, e3=C, gro=2 * C, yo=C, ll=2 * C),
}
for _b in range(8):
    SCRATCH["ps%d" % _b] = ("psum", [128, 512], "float32")
for _r in range(3):
    for _n in ("so", "ro", "la"):
        SCRATCH["%sR%d" % (_n, _r)] = ("sbuf", [128, 2 * K if _n == "so" else K], "uint16")
        SCRATCH["%sM%d" % (_n, _r)] = ("sbuf", [128, 11], "uint16")
        SCRATCH["%sQ%d" % (_n, _r)] = ("sbuf", [128, HALF], "float8_e4m3fn_x4")
        SCRATCH["%sS%d" % (_n, _r)] = ("sbuf", [128, HALF], "uint8")
LOADS = ["lt", "rt", "x", "u", "lv", "wc", "ws", "v"]
SEMAPHORES = (["cv", "cs", "ct", "cp", "ls", "outs"] + ["ld_" + n for n in LOADS]
              + ["a%s%d" % (n, r) for n in "RMCS" for r in range(3)])


def route(topo, core, partner):
    ok = [c for c in topo.cores_of(core) if c != core and topo.may_write(c, partner)]
    near = [c for c in ok if topo.die(c) == topo.die(core)]
    far = [c for c in ok if topo.die(c) != topo.die(core)]
    return near[0], far[0], near[1]


def bits(engines):
    return sum(1 << e for e in engines)


def sent_on(kind, rd):
    return 16 if kind == "S" or (kind == "R" and rd) else 8


def relay_program(g, core, T, topo, rank):
    src, sent = T.cores[rank], 0
    for rd, s in enumerate(STEP):
        dst = T.cores[rank ^ s]
        a, b, c = route(topo, src, dst)
        if core not in (a, b, c):
            continue
        rid, pid = topo.addr(dst, core)
        eng = topo.engines(core, dst)[:8]
        jobs = {a: [("R", "R", 0, K), ("C", "Q", 0, 88)], b: [("C", "Q", 88, HALF)], c: [("M", "M", 0, 11), ("S", "S", 0, HALF)]}[core]
        for sem, buf, lo, hi in jobs:
            g.wait_ge(T.sem["a%s%d" % (sem, rd)], sent_on(sem, rd))
            o, i = T["la%s%d" % (buf, rd)][:, lo:hi], T["ro%s%d" % (buf, rd)][:, lo:hi]
            if buf == "Q":
                o, i = o.bitcast(dt.uint8), i.bitcast(dt.uint8)
            g.remote_dma(o, i, T.sem["a%s%d" % (sem, rd)], T.sem["ls"], pid, rid, bits(eng))
            sent += len(eng)
    if sent:
        g.wait_ge(T.sem["ls"], sent)


def rank_program(g, core, T, topo):
    rank = T.rank_of(core)
    if rank is None:
        for c in topo.cores_of(core):
            if T.rank_of(c) is not None:
                relay_program(g, core, T, topo, T.rank_of(c))
        return

    eng = {"v": g.vector, "s": g.scalar, "t": g.tensor, "p": g, "y": g.sync}
    done = {"v": "cv", "s": "cs", "t": "ct", "p": "cp"}
    count = {"cv": 0, "cs": 0, "ct": 0, "cp": 0, "outs": 0, "ls": 0}
    known = {q: {} for q in eng}
    uses = {}
    clocks = {}

    def meet(a, b):
        if a[1] >= b[2] or b[1] >= a[2]:
            return False
        return not (a[3] == b[3] and a[3] > 1 and (a[1] - b[1]) % a[3])

    def before(q, reads, writes):
        need = {}
        for w, regs in ((False, reads), (True, writes)):
            for r in regs:
                ps = r[0][:2] == "ps"
                for (o, ow, oq, tok) in uses.get(r[0], []):
                    if (w or ow or (ps and oq != q)) and meet(r, o):
                        need[tok[0]] = max(need.get(tok[0], 0), tok[1])
        k = known[q]
        for s in sorted(need, key=lambda s: s in ("cv", "cs", "ct", "cp")):
            if k.get(s, 0) < need[s]:
                eng[q].wait_ge(T.sem[s], need[s])
                k[s] = need[s]
                for a, b in clocks.get((s, need[s]), {}).items():
                    k[a] = max(k.get(a, 0), b)

    def note(q, tok, reads, writes):
        clocks[tok] = dict(known[q])
        for r in writes:
            uses[r[0]] = [u for u in uses.get(r[0], []) if not (r[3] in (1, u[0][3]) and r[1] <= u[0][1] and u[0][2] <= r[2] and (u[0][1] - r[1]) % r[3] == 0)]
        for w, regs in ((False, reads), (True, writes)):
            for r in regs:
                uses.setdefault(r[0], []).append((r, w, q, tok))

    def run(q, fn, reads, writes):
        before(q, reads, writes)
        s = done[q]
        count[s] += 1
        fn().then_inc(T.sem[s], 1)
        note(q, (s, count[s]), reads, writes)

    def load(q, sem, out, in_, reg):
        before(q, [], [reg])
        eng[q].dma_start(out, in_).then_inc(T.sem[sem], 16)
        note(q, (sem, 16), [], [reg])

    def store(q, out, in_, reg):
        before(q, [reg], [])
        eng[q].dma_start(out, in_).then_inc(T.sem["outs"], 16)
        count["outs"] += 16

    def R(name, lo=0, hi=None, step=1):
        return (name, lo, SCRATCH[name][1][1] if hi is None else hi, step)

    def W(name, lo=0, hi=K):
        return ("wi", WI[name] + lo, WI[name] + hi, 1)

    def U(name, lo=0, hi=K):
        return ("wu", WU[name] + lo, WU[name] + hi, 1)

    def Fl(name, lo=0, hi=K):
        return ("wf", WF[name] + lo, WF[name] + hi, 1)

    def ap(r):
        return T[r[0]][:, r[1]:r[2]] if r[3] == 1 else T[r[0]][:, r[1]:r[2]:r[3]]

    def src(r, ind):
        return ap(r) if ind is None else ap(r).indirect(ap(ind))

    def given(*rs):
        return [r for r in rs if r is not None]

    def tt(out, in0, in1, op, ind=None):
        run("v", lambda: g.vector.tensor_tensor(ap(out), src(in0, ind), ap(in1), op), given(in0, in1, ind), [out])

    def ts(out, in0, s1, op0, s2=None, op1=None):
        if op1 is None:
            run("v", lambda: g.vector.tensor_scalar(ap(out), ap(in0), s1, None, op0), [in0], [out])
        else:
            run("v", lambda: g.vector.tensor_scalar(ap(out), ap(in0), s1, s2, op0, op1), [in0], [out])

    def cp(out, in_, ind=None):
        run("v", lambda: g.vector.tensor_copy(ap(out), src(in_, ind)), given(in_, ind), [out])

    def put(out, ind, in_):
        run("v", lambda: g.vector.tensor_copy(ap(out).indirect(ap(ind)), ap(in_)), [in_, ind], [out])

    def fill(out, c):
        run("v", lambda: g.vector.memset(ap(out), c), [], [out])

    def act(out, in_, ind=None, func=Act.Copy, scale=1.0):
        if scale == 1.0:
            run("s", lambda: g.scalar.activation(ap(out), src(in_, ind), func), given(in_, ind), [out])
        else:
            run("s", lambda: g.scalar.activation(ap(out), src(in_, ind), func, scale=scale), given(in_, ind), [out])

    def shift(out, in_, scale, bias):
        run("s", lambda: g.scalar.activation(ap(out), ap(in_), Act.Identity, bias=bias, scale=scale), [in_], [out])

    def scan(out, d0, d1, op0, op1):
        run("v", lambda: g.vector.tensor_tensor_scan(ap(out), ap(d0), ap(d1), 0.0, op0, op1), [d0, d1], [out])

    def quant(name, tile, lo, hi, q=None, s=None):
        q, s = q or "q" + name, s or "s" + name
        t = R(tile, 4 * lo, 4 * hi)
        run("v", lambda: g.vector.quantize_mx(T[q][:, lo:hi], T[s][:, lo:hi], ap(t)), [t], [R(q, lo, hi), R(s, lo, hi)])

    def mm(bank, w, wlo, q, s, lo, hi):
        p, wq, wsc = "ps%d" % bank, "q" + w, "s" + w
        run("t", lambda: g.tensor.matmul_mx(T[p][:, 0:hi - lo], T[wq][:, wlo:wlo + 128], T[wsc][:, wlo:wlo + 128], T[q][:, lo:hi], T[s][:, lo:hi], True, True),
            [R(wq, wlo, wlo + 128), R(wsc, wlo, wlo + 128), R(q, lo, hi), R(s, lo, hi)], [R(p)])

    def arrive(name, sem, n):
        note("p", (sem, n), [], [R(name)])
        clocks[(sem, n)] = {}

    def send(rds, fn, n):
        before("p", rds, [])
        fn()
        count["ls"] += n

    def masked(out, row):
        scan(out, row, R("dm"), Op.add, Op.mult)

    def pick(out, row):
        scan(out, R("km"), row, Op.mult, Op.add)

    def ends(name):
        return (name, 15, C, 16)

    def col16(out, x):
        w = x[2] - x[1]
        ts(W("t1", 0, w), x, float(C), Op.is_ge, -float(C), Op.mult)
        tt(W("t2", 0, w), x, W("t1", 0, w), Op.add)
        cp(out, W("t2", 0, w))

    def iota(out, pattern, base, cm):
        if out[0] in ("kr", "rc"):
            run("p", lambda: g.iota(ap(out), pattern, base, cm, allow_small_or_imprecise_dtypes=True), [], [out])
        else:
            run("p", lambda: g.iota(ap(out), pattern, base, cm), [], [out])

    load("y", "ld_lt", T["lw"][:], T["lt"][:], R("lw"))
    load("s", "ld_rt", T["rw"][:], T["rt"][:], R("rw"))
    load("y", "ld_u", T["ut"][:], T["u"][:], R("ut"))
    load("s", "ld_x", T["xt"][:], T["x"][:], R("xt"))
    load("y", "ld_lv", T["lvt"][:], T["lv"][:], R("lvt"))
    load("y", "ld_wc", T["qw"][:, 0:512].bitcast(dt.uint8), T["wc"][:, 0:2048], R("qw"))
    load("y", "ld_ws", T["sw"][:, 0:512], T["ws"][:, 0:512], R("sw"))
    load("y", "ld_v", T["vt"][:], T["v"][:], R("vt"))

    iota(W("x"), [[0, K]], 0, 1)
    iota(R("kr"), [[0, K], [1, 16]], 0, 0)
    iota(W("i32"), [[32, K]], 0, 0)
    iota(W("mm"), [[16, K]], 0, 0)
    iota(R("ui"), [[1, 4], [16, 8]], 0, 0)
    iota(R("rc"), [[1, C]], 0, 0)
    fill(R("none"), float(C))
    fill(R("ones"), 1.0)
    fill(R("km"), 1.0)
    fill(W("SS"), C)
    ts(W("t1"), W("x"), 31, Op.bitwise_and)
    ts(W("t2"), W("x"), 15, Op.bitwise_and)
    fill(R("km", 0, C, 16), 0.0)
    act(R("pw0", 0, C), R("none"))
    act(R("tw0", C, 2 * C), R("none"), scale=0.0)
    act(R("tw1", C, 2 * C), R("none"), scale=0.0)
    act(R("kmb"), R("km"))
    act(R("wb", 2 * C, 3 * C), R("none"), scale=0.0)
    cp(Fl("px", 0, 8), W("t2", 0, 8))
    tt(W("mt"), W("t1"), W("i32"), Op.add)
    px = Fl("px", 0, 1)
    shift(R("one", 0, C), R("none"), 0.0, 1.0)
    shift(R("one", C, 512), R("none", 0, 160), 0.0, 1.0)
    run("v", lambda: g.vector.tensor_scalar(T["dm"][:], T["kr"][:], ap(px), None, Op.is_equal), [R("kr"), px], [R("dm")])
    act(R("dmb"), R("dm"))
    cp(U("LX"), W("mt"))
    tt(W("CB"), W("t2"), W("mm"), Op.add)
    cp(R("ux"), R("ui"))
    ts(W("CB", K, 2 * K), W("CB"), float(C), Op.add)
    ts(W("c704"), W("CB"), 2.0 * C, Op.add)

    ts(W("mi"), R("rw"), 1024.0, Op.mult)
    cp(U("OLs"), R("lw"))
    tt(Fl("pk"), W("mi"), R("lw"), Op.add)
    for q in range(K):
        o, i = R("ex", 32 * q, 32 * q + 32), Fl("pk", q, q + 1)
        run("s", lambda: g.scalar.activation(ap(o), T["ones"][:], Act.Copy, scale=ap(i)), [R("ones"), i], [o])

    def replicas(k):
        a, e = 128 * k, 8 * k
        run("v", lambda: g.vector.tensor_copy(T["qur"][:, a:a + 256].bitcast(dt.uint32), T["qu"][:, 0:128].bitcast(dt.uint32).indirect(T["ux"][:, e:e + 16])),
            [R("qu"), R("ux")], [R("qur", a, a + 256)])
        run("s", lambda: g.scalar.activation(T["sur"][:, a:a + 256], T["su"][:, 0:128].indirect(T["ux"][:, e:e + 16]), Act.Copy),
            [R("su"), R("ux")], [R("sur", a, a + 256)])

    def parents(pw, ol, *between):
        f = list(between) + [lambda: None] * 2
        put(R(pw), ol, R("rc"))
        f[0]()
        masked(R("e1"), R(pw, 0, C))
        f[1]()
        pick(R("e2"), R("e1"))
        cp(W("par"), ends("e2"))

    def start():
        quant("u", "ut", 0, 128)
        replicas(0)

    lists = [U("OLs"), None]
    parents("pw0", lists[0], start)
    quant("x", "xt", 0, C)
    run("v", lambda: g.vector.transpose(T["tr"][:], T["ex"][:]), [R("ex")], [R("tr")])
    act(R("lrf"), R("tr"), U("LX"), scale=FR)
    cp(W("LR0"), R("lw"))
    cp(W("LR0", K, 2 * K), R("rw"))
    col16(U("OLC0"), W("LR0"))
    tt(W("dlp"), W("LR0"), W("par"), Op.subtract)
    for b in range(4):
        run("p", lambda: g.affine_select(T["et"][:, 512 * b:512 * b + 512], T["one"][:], [[-1, 512]], Op.is_equal, 0.0, b, 4),
            [R("one")], [R("et", 512 * b, 512 * b + 512)])

    def windows():
        for t in range(4):
            act(R("win", 704 * t, 704 * t + C), R("xt", t, 4 * C, 4), scale=0.5)

    def scores(lo, hi, bank):
        for k in range(2):
            mm(bank + k, "ur", 128 * k, "qx", "sx", lo, hi)
        act(R("sg0", lo, hi), R("ps%d" % bank, 0, hi - lo), func=Act.Sign, scale=-1.0)

    def signs(lo, hi, bank):
        ts(R("pf0", lo, hi), R("ps%d" % (bank + 1), 0, hi - lo), 0.0, Op.is_gt, 0.5, Op.mult)
        scan(R("e1s", lo, hi), R("ps%d" % bank, 0, hi - lo), R("dm", lo, hi), Op.add, Op.mult)
        tt(R("lrs", lo, hi), R("lrf", lo, hi), R("sg0", lo, hi), Op.add)
        scan(R("e2s", lo, hi), R("kmb", lo, hi), R("e1s", lo, hi), Op.mult, Op.add)
        ts(W("A", lo // 16, hi // 16), ("e2s", lo + 15, hi, 16), 0.0, Op.is_gt)

    def step(rd, j, more=None, rest=None):
        lr, ln = W("LR%d" % j, 0, 44), W("LR%d" % (1 - j), 0, 44)
        l, r = W("LR%d" % j), W("LR%d" % j, K, 2 * K)
        tw, pf = "tw%d" % j, R("pf%d" % j)
        sl, sr = U("SL0", 0, K), U("SL0", K, 2 * K)
        if j == 0:
            tt(R(tw, 0, C), pf, R("lrs"), Op.add, U("OLC0"))
            act(R("twb"), R(tw, 0, C))
            more()
        else:
            tt(R(tw, 0, C), pf, R("lrs"), Op.add, U("OL1"))
            act(R("twb"), R(tw, 0, C))
            act(R("wb", 0, C), R("wa", 0, 2 * C), sl)
            act(R("wb", C, 2 * C), R("wa", 0, 2 * C), sr)
        own = ends("e2b")

        def ownmask():
            scan(R("e1b"), R("twb"), R("dmb"), Op.add, Op.mult)

        def picked():
            scan(R("e2b"), R("kmb"), R("e1b"), Op.mult, Op.add)

        if j == 1:
            put(R(tw, 2 * C, 4 * C), U("OL1"), R("a1"))
            shift(R("wb", 3 * C, 4 * C), R(tw, 2 * C, 3 * C), 1.0 / F10, 1.0 / F10)
            ownmask()
            tt(W("dlp"), l, W("c704"), Op.subtract)
            picked()
            tt(W("E"), r, l, Op.subtract)
            ts(W("A"), own, 0.0, Op.is_lt)
            tt(W("Q"), l, W("CB"), Op.subtract)
        tt(W("aM"), W("A"), W("dlp"), Op.mult)
        if j == 0:
            tt(W("E"), r, l, Op.subtract)
        tt(W("o"), W("aM"), W("par") if j == 0 else W("c704"), Op.add)
        if j == 0:
            tt(W("Q"), l, W("CB"), Op.subtract)
        cp(U("O"), W("o"))
        tt(R("gg"), R(tw, 0, (2 if j == 0 else 3) * C), R("dm"), Op.mult, U("O"))
        tt(W("Q", K, 2 * K), W("o"), W("CB"), Op.subtract)
        oth = ends("e3")
        if j == 0:
            ownmask()
            pick(R("e3"), R("gg"))
            picked()
            ts(W("I"), oth, 1.0, Op.add, 2.0 ** 22, Op.mult)
        ts(Fl("tP"), own, 0.0, Op.is_ge, 1.5, Op.add)
        ts(Fl("tA"), own, 0.0, Op.is_ge, 1.0, Op.add)
        ts(Fl("tN"), own, 1.0, Op.is_ge, -1.0, Op.add)
        ts(Fl("tQ"), own, 1.5, Op.is_ge, -1.0, Op.add)
        if j == 0:
            if rd == 0:
                tt(R("wa", 0, C), R("lrf"), R("wa", 3 * C, 4 * C), Op.subtract)
                act(R("wa", 2 * C, 3 * C), R("wa", 0, C), scale=F10)
            rest()
        else:
            pick(R("e3"), R("gg"))
        ts(W("SS", K, 2 * K), W("Q", K, 2 * K), -1.0, Op.mult, -float(C), Op.add)
        if j == 1:
            ts(W("I"), oth, 1.0, Op.add, 2.0 ** 22, Op.mult)
        tt(W("vA"), oth, Fl("tA"), Op.is_ge)
        tt(W("vN"), oth, Fl("tN"), Op.is_lt)
        ts(W("LH"), W("I"), 1023, Op.bitwise_and)
        ts(W("LH", K, 2 * K), W("I"), 10, Op.arith_shift_right, 1023, Op.bitwise_and)
        tt(W("F", K, 2 * K), oth, Fl("tP"), Op.is_ge)
        tt(W("F"), oth, Fl("tQ"), Op.is_lt)
        tt(W("F", 2 * K, 3 * K), W("vA"), W("vN"), Op.add)
        tt(W("D", 0, 44), W("LH", 0, 44), lr, Op.subtract)
        tt(W("E", K, 2 * K), l, W("LH", K, 2 * K), Op.subtract)
        fa, fb = W("F", K, 3 * K), W("F", 0, 2 * K)
        n = [lambda: tt(W("N1", 0, 44), fa, W("Q", 0, 44), Op.mult), lambda: tt(W("N2", 0, 44), fb, W("SS", 0, 44), Op.mult),
             lambda: tt(W("N3", 0, 44), W("N1", 0, 44), W("N2", 0, 44), Op.add), lambda: tt(W("N4", 0, 44), W("CB", 0, 44), W("N3", 0, 44), Op.add),
             lambda: cp(U("SL%d" % j, 0, 44), W("N4", 0, 44))]
        if j == 0:
            n[0](), n[1]()
        tt(W("M1", 0, 44), fa, W("D", 0, 44), Op.mult)
        tt(W("M2", 0, 44), fb, W("E", 0, 44), Op.mult)
        n[2 if j == 0 else 0]()
        tt(W("M3", 0, 44), W("M1", 0, 44), W("M2", 0, 44), Op.add)
        n[3 if j == 0 else 1]()
        tt(ln, lr, W("M3", 0, 44), Op.add)
        if j == 0:
            n[4]()
            cp(U("OL1"), W("LR1"))
            tt(R("a1"), R("wa", 2 * C, 4 * C), R("sg1"), Op.add, sr)
            tt(R("lrs"), R("wa", 0, 2 * C), R("a1"), Op.add, sl)
        else:
            n[2]()
            cp(R("soR%d" % rd), ln)
            n[3]()
            n[4]()

    for rd in range(3):
        last = rd == 2
        partner = T.cores[rank ^ STEP[rd]]
        ra, rb, rc = route(topo, core, partner)

        def to(relay, lo, n):
            return bits(topo.engines(core, relay)[lo:lo + n])

        def remote(buf, sem, relay, lo, n, a=0):
            rid, pid = topo.addr(relay, core)
            o, i = T["ro%s%d" % (buf, rd)], T["so%s%d" % (buf, rd)]
            send([R("so%s%d" % (buf, rd))],
                 lambda: g.remote_dma(o[:], i[:, a:], T.sem["a%s%d" % (sem, rd)], T.sem["ls"], pid, rid, to(relay, lo, n)), n)

        scores(0, C if rd == 0 else HALF, 0)
        if rd > 0:
            signs(HALF, C, 2)
        signs(0, C if rd == 0 else HALF, 0)

        def more():
            for t in range(0 if rd == 0 else 4):
                act(R("win", 704 * t + C, 704 * t + C + HALF), R("ps%d" % (4 + t), 0, HALF), scale=0.5)
            if rd == 0:
                shift(R("sgt"), R("lrf"), 2.0 ** 12, -511.0 / 1024)
                shift(R("a1"), R("sgt"), 1.0, 1.5 * 2.0 ** 23)
                shift(R("sg1"), R("a1"), 1.0, -1.5 * 2.0 ** 23)
                act(R("wa", 3 * C, 4 * C), R("sg1"), scale=FR * F10)
                act(R("wa", C, 2 * C), R("sg1"), scale=FR)
                replicas(2)
            for k in range(2, 4):
                mm(2 + k, "ur", 128 * k, "qx", "sx", 0, C)
            act(R("sg1"), R("ps4", 0, C), func=Act.Sign, scale=-1.0)

        def rest():
            act(R("sgt"), R("ps5", 0, C), func=Act.Sign)
            act(R("pf1", 0, C), R("sgt"), func=Act.Relu, scale=0.5)
            act(R("pf1", C, 2 * C), R("sgt"), func=Act.Relu, scale=0.5)
            act(R("tw1", 2 * C, 3 * C), R("none"), scale=0.0)
            if not last:
                act(R("pw0", 0, C), R("none"))
        step(rd, 0, more, rest)
        step(rd, 1)
        remote("R", "R", ra, 0, sent_on("R", rd), K)
        lists[0], lists[1] = R("soR%d" % rd, 0, K), R("soR%d" % rd, K, 2 * K)
        part = lambda r, lo, hi: (r[0], r[1] + lo // 16, r[1] + hi // 16, 1)
        for h, (lo, hi) in enumerate(CHUNKS):
            for t in range(4):
                if h == 0 and rd == 0:
                    act(R("win", 704 * t + C, 704 * t + 2 * C), R("lvt", t, 4 * C, 4), scale=0.5)
            if h == 0:
                windows()
            for t in range(4):
                act(R("gl", C * t + lo, C * t + hi), R("win", 704 * t, 704 * t + 704), part(lists[0], lo, hi))
                tt(R("zt", 4 * lo + t, 4 * hi, 4), R("win", 704 * t, 704 * t + 704), R("gl", C * t + lo, C * t + hi), Op.add, part(lists[1], lo, hi))
            quant("z", "zt", lo, hi)
            for b in range(4):
                mm(4 * h + b, "w", 128 * b, "qz", "sz", lo, hi)
        act(R("ll", 0, C), R("wb", 0, 2 * C), U("SL1", 0, K))
        for h, (lo, hi) in enumerate(CHUNKS):
            for b in range(4):
                o, i = R("hp", C * b + lo, C * b + hi), R("ps%d" % (4 * h + b), 0, hi - lo)
                if b % 2 == 0 or (h, b) == (1, 3):
                    ts(o, i, 0.03125, Op.mult)
                else:
                    act(o, i, scale=0.03125)
            if h == 0:
                act(R("ll", C, 2 * C), R("ll", 0, C))
        arrive("laR%d" % rd, "aR%d" % rd, 8)
        tt(R("gg"), R("ll"), R("dm"), Op.mult, R("laR%d" % rd))
        pick(R("e3"), R("gg"))
        ts(W("mi"), ends("e3"), 2.0 ** 22, Op.mult)
        ts(W("mt"), ends("e3"), float(C) * FR, Op.is_ge, -float(C), Op.mult)
        tt(W("mm"), W("mi"), W("mt"), Op.add)
        cp(U("MO"), W("mm"))
        cp(R("soM%d" % rd), W("mm", 11, 22))
        remote("M", "M", rc, 8, sent_on("M", rd))
        for b in range(4):
            o, i, n = R("gt", b, 4 * HALF, 4), R("hp", C * b, C * b + C), U("MO", 0, 11)
            if b % 2 == 0:
                cp(o, i, n)
            else:
                act(o, i, n)
        q, s = "soQ%d" % rd, "soS%d" % rd
        quant("", "gt", 0, HALF, q, s)

        def codes():
            tr = []
            for relay, lo, e in ((ra, 0, 0), (rb, 88, 8)):
                rid, pid = topo.addr(relay, core)
                tr.append(RemoteDMATransfer(dst_ids=[DstId(rid=rid, pnc=pid)], dma_engine_mask=to(relay, e, 8), remote_sem=T.sem["aC%d" % rd],
                                            src=T[q][:, lo:lo + 88].bitcast(dt.uint8), dst=T["roQ%d" % rd][:, lo:lo + 88].bitcast(dt.uint8)))
            g.remote_dma_fused(tr, local_sem=T.sem["ls"])
        send([R(q)], codes, 16)
        remote("S", "S", rc, 0, sent_on("S", rd))
        act(R("wa", C, 2 * C), R("wb"), U("SL1", K, 2 * K))
        act(R("wa", 0, C), R("ll", 0, C))
        if not last:
            act(R("wa", 2 * C, 4 * C), R("wa", 0, 2 * C), scale=F10)
            parents("pw0", lists[0], lambda: ts(W("t1"), W("LR0"), float(C), Op.is_ge, -float(C), Op.mult),
                    lambda: tt(W("t2"), W("LR0"), W("t1"), Op.add))
            cp(U("OLC0"), W("t2"))
            tt(W("dlp"), W("LR0"), W("par"), Op.subtract)
        if rd == 0:
            quant("e", "et", 0, 512)
        if not last:
            tt(R("lrf"), R("wa", 0, C), R("wa", 3 * C, 4 * C), Op.add)
        else:
            act(R("gro"), R("wa", 0, 2 * C), scale=2.0 ** 22)
            store("y", T["gr"][:, :], T["gro"][0:128:16, :], R("gro"))
            quant("v", "vt", 0, 128)
        arrive("laM%d" % rd, "aM%d" % rd, 8)
        own = R("laM%d" % rd, 0, 11)
        for b in range(4):
            x = R("xt", 4 * HALF + b, 4 * C, 4)
            tt(x, R("hp", C * b, C * b + C), x, Op.add, own)
        quant("x", "xt", HALF, C)
        if not last:
            for b in range(4):
                act(R("win", 704 * b + C + HALF, 704 * b + 2 * C), R("hp", C * b, C * b + C), own, scale=0.5)
        else:
            mm(0, "v", 0, "qx", "sx", HALF, C)
            act(R("yo", HALF, C), R("ps0", 0, HALF))
            store("y", T["oc"][:, 4 * HALF:4 * C], T["qx"][:, HALF:C].bitcast(dt.uint8), R("qx", HALF, C))
            for k in range(4):
                store("y", T["osc"][4 * k:4 * k + 4, HALF:C], T["sx"][32 * k:32 * k + 4, HALF:C], R("sx", HALF, C))
            store("y", T["y"][:, HALF:C], T["yo"][:, HALF:C], R("yo", HALF, C))
        arrive("laQ%d" % rd, "aC%d" % rd, 16)
        arrive("laS%d" % rd, "aS%d" % rd, 8)
        for b in range(4):
            mm(4 + b, "e", 128 * b, "laQ%d" % rd, "laS%d" % rd, 0, HALF)
        if not last:
            scores(HALF, C, 2)
        for b in range(4):
            x = R("xt", b, 4 * HALF, 4)
            tt(x, R("ps%d" % (4 + b), 0, HALF), x, Op.add)
        quant("x", "xt", 0, HALF)
    mm(1, "v", 0, "qx", "sx", 0, HALF)
    act(R("yo", 0, HALF), R("ps1", 0, HALF))
    store("y", T["oc"][:, 0:4 * HALF], T["qx"][:, 0:HALF].bitcast(dt.uint8), R("qx", 0, HALF))
    for k in range(4):
        store("s" if k % 2 else "y", T["osc"][4 * k:4 * k + 4, 0:HALF], T["sx"][32 * k:32 * k + 4, 0:HALF], R("sx", 0, HALF))
    store("s", T["y"][:, 0:HALF], T["yo"][:, 0:HALF], R("yo", 0, HALF))
    for s in sorted(count):
        g.wait_ge(T.sem[s], count[s])
